import numpy as np, ml_dtypes
CORES = [2,3,42,43,82,83,122,123]
N = 8
BF = ml_dtypes.bfloat16
A, W, HM, RO, MU = 512, 4096, 1, 4, 8
n = A // 4
def view(j, c):
    return np.where(c < 0, W, (((c * (MU * j + 5)) >> 5) + 37 * j) & (W - 1))
def worth(tab, j, b):
    x = tab[:, view(j[None, :], b)]
    return np.add.reduce(np.maximum.accumulate(x[:, ::-1], axis=1)[:, ::-1], axis=0)
def pack(x, b, p):
    return {"sight": x.reshape(N, 128, W).astype(np.float32).astype(BF), "bun": np.ascontiguousarray(b.reshape(N, 128, A)).astype(np.int32), "pots": p.astype(np.int32)}
def looks(rng):
    return (rng.integers(0, 256, (N, 8, 16, W)) * rng.integers(1, 9, (N, 8, 1, W))) >> 3
def some(rng, goods, shares):
    return np.where(rng.random((N, 8, 16, A)) < rng.choice(np.array(shares), (N, 8, 1, A)), goods, -1)
def setup_inputs(rng):
    b = some(rng, rng.integers(0, 4096, (N, 8, 16, A)), [0.05, 0.2, 0.4, 0.7, 1.0])
    p = np.where(rng.random((N, 8, n)) < 0.85, rng.integers(0, 4096, (N, 8, n)), -1)
    return pack(looks(rng), b, p)
def setup_inputs_spread(rng):
    x = np.floor(np.exp2(8 * rng.random((N, 8, 1, W)) * rng.random((N, 8, 16, W)) ** 0.5)).astype(np.int64) - 1
    x = np.where(rng.random((N, 8, 16, W)) < 0.02, 255, np.clip(x, 0, 255))
    e = rng.choice(np.array([0.5, 1.0, 3.0, 6.0]), (N, 8, 1, A))
    b = some(rng, np.minimum((4096 * rng.random((N, 8, 16, A)) ** e).astype(np.int64), 4095), [0.05, 0.15, 0.5, 0.95])
    p = np.minimum((4096 * rng.random((N, 8, n)) ** rng.choice(np.array([0.3, 1.0, 4.0]), (N, 8, 1))).astype(np.int64), 4095)
    return pack(x, b, np.where(rng.random((N, 8, n)) < 0.9, p, -1))
def setup_inputs_ends(rng):
    see = view(np.arange(A), np.int64(4095))
    x = 255 * (rng.random((N, 8, 16, W)) < rng.choice(np.array([0.05, 0.3, 0.6, 0.95]), (N, 8, 1, W))).astype(np.int64)
    x[:, :, 0, see[0::4]] = 255
    far = np.array([0, A - 67, A - 66, A - 65, A - 4, A - 3, A - 2, A - 1]); x[..., see[far]] = 255
    b = some(rng, np.int64(4095), [0.0, 0.1, 0.5, 1.0])
    own = (rng.random((N, 8, 1, A)) < 0.33) & (np.arange(A) % 4 != 0)
    b = np.where(own, rng.integers(0, 4096, (N, 8, 16, A)), b)
    b[:, :, 3, 0::4] = 4095; b[..., 0] = 4095; b[..., A - 67:A - 64] = -1; b[..., A - 4] = -1
    end = np.where(rng.random((N, 8, 1, 3)) < 0.5, 4095, -1); end[N - 1, 7] = np.array([-1, 4095, -1]); end[0, 7] = np.array([-1, -1, 4095]); end[1, 7] = np.array([4095, -1, -1])
    b[..., A - 3:] = end
    p = np.where(rng.random((N, 8, n)) < 0.7, np.where(rng.random((N, 8, n)) < 0.6, 4095, -1), rng.integers(0, 4096, (N, 8, n)))
    p[..., 0] = 4095; p[..., n - 1] = 4095
    return pack(x, b, p)
def setup_inputs_corners(rng):
    x = looks(rng); b = rng.integers(0, 4096, (N, 8, 16, A)); p = rng.integers(0, 4096, (N, 8, n)); d = np.arange(16)[:, None]
    for r in range(N):
        mode = rng.permutation(8)
        for g in range(8):
            m = int(mode[g])
            if m == 0: b[r, g] = -1
            if m == 2: b[r, g, :15] = -1
            if m == 3: b[r, g, 1:] = -1
            if m == 4:
                c = int(b[r, g, 0, 0]); b[r, g] = np.where(rng.random((16, A)) < rng.random((1, A)), c, -1); p[r, g] = c
            if m == 5: b[r, g] = np.where(rng.random((1, A)) < 0.5, b[r, g], -1)
            if m == 6:
                k = rng.choice(np.array([0, 1, 15, 16]), (1, A)); low = rng.random((1, A)) < 0.5
                b[r, g] = np.where(np.where(low, d < k, d >= 16 - k), b[r, g], -1); p[r, g] = -1
            if m == 7: x[r, g] = 0
    return pack(x, b, p)
def calls(rng):
    return np.argsort(rng.random((N, 3, n)), axis=-1) + n * rng.integers(0, W // n, (N, 3, n))
def setup_inputs_ties(rng):
    base = rng.choice(np.array([0, 1, 127, 254]), (N, 8, 1, 1)); base[0, 0] = 0; base[0, 7] = 254; base[N - 1, 7] = 254
    x = base + (rng.random((N, 8, 16, W)) < 0.125)
    few = rng.integers(0, 4096, 32); few[0] = 0; few[1] = 4095
    b = some(rng, few[rng.integers(0, 32, (N, 8, 16, A))], [0.0, 0.1, 0.3, 0.6])
    p = np.where(rng.random((N, 8, n)) < 0.9, few[rng.integers(0, 32, (N, 8, n))], -1)
    full = rng.integers(0, 4096, (N, 16, A)); b3 = np.where(rng.random((N, 1, A)) < 0.5, full, -1)
    b3[:, :, 0::4] = full[:, :, 0::4]
    b3[:, 0:3, 0::4] = calls(rng)
    x[:, 3] = 100; b[:, 3] = b3
    for m in range(3):
        bm = rng.integers(0, 4096, (N, 16, A)); bm[:, 0:3, 0::4] = calls(rng); bm[:, :, m + 1::4] = -1
        x[:, 4 + m] = 100; b[:, 4 + m] = bm
    return pack(x, b, p)
def check_inputs(d):
    bad = []
    for k, lo, hi in (("sight", 0, 255), ("bun", -1, 4095), ("pots", -1, 4095)):
        v = np.asarray(d[k]).astype(np.float64)
        if not np.all((v >= lo) & (v <= hi) & (v == np.floor(v))): bad.append("range of " + k)
    return bad
def reference(sight, bun, pots):
    tab = np.zeros((N, 8, 16, W + 1), np.int32); tab[..., :W] = sight.astype(np.float32).reshape(N, 8, 16, W).astype(np.int32)
    bn = bun.astype(np.int64).reshape(N, 8, 16, A); p = pots.astype(np.int64); val = np.zeros((N, 8, A), np.int64)
    for r in range(N):
        for g in range(8): val[r, g] = worth(tab[r, g], np.arange(A), bn[r, g])[0]
    place = np.arange(16)[:, None]
    for t in range(RO):
        u = 4 * np.arange(n) + (t & 3); nbn = bn.copy(); nval = val.copy(); npots = np.zeros((N, 8, n), np.int64)
        for r in range(N):
            for g in range(8):
                old = bn[r, g][:, u]; s = old.copy(); s[15] = p[r, g]
                best = np.zeros(n, np.int64); who = np.full(n, -1); riv = []
                for m in range(3):
                    q = r if m < HM else (r + 1 + (t + m - HM) % (N - 1)) % N
                    j = 4 * ((old[m] + val[r, g, u] + 13 * t) & (n - 1)) + ((t + 1 + m) & 3)
                    first = np.zeros(n, bool); first[np.unique(j, return_index=True)[1]] = True
                    sv = worth(tab[q, g], j, s)
                    e = np.where(first, np.add.reduce((sv > val[q, g, j]).astype(np.int64), axis=0), 0)
                    who = np.where(e > best, m, who); best = np.maximum(best, e); riv.append((q, j, sv))
                new = s.copy()
                for m in range(3):
                    q, j, sv = riv[m]; c = np.flatnonzero(who == m); jc = j[c]
                    nbn[q, g][:, jc] = np.where(place >= best[c] - 1, s[:, c], -1); nval[q, g, jc] = sv[best[c] - 1, c]
                    new[:, c] = bn[q, g][:, jc]
                nbn[r, g][:, u] = new; nval[r, g, u] = worth(tab[r, g], u, new)[0]
                npots[(r + 1) % N, g] = np.where(best >= 2, s[np.maximum(best - 2, 0), np.arange(n)], old[15])
        bn, val, p = nbn, nval, npots
    return {"yb": bn.reshape(N, 128, A).astype(np.float32), "yv": val.astype(np.float32), "yp": p.astype(np.float32)}

@@ -1,0 +1,714 @@
+import numpy as np
+from concourse.bass import DstId, RemoteDMATransfer
+from concourse.mybir import AluOpType, ActivationFunctionType
+
+N = 8
+OFF = 257
+MASK = 4095 + (1 << 20)
+SH = 2047.0
+F32, BF, I32, U16, F16 = "float32", "bfloat16", "int32", "uint16", "float16"
+
+SCRATCH = {
+    "xs": ("dram", [8, 128, 512], BF), "xr": ("dram", [8, 128, 512], BF),
+    "bs": ("dram", [8, 128, 64], I32), "br": ("dram", [8, 128, 64], I32),
+    "qs": ("dram", [128, 8], I32), "qr": ("dram", [8, 128, 8], I32),
+    "ys": ("dram", [8, 128, 64], F32), "yr": ("dram", [8, 128, 64], F32),
+    "vs": ("dram", [8, 128, 4], F32), "vr": ("dram", [8, 128, 4], F32),
+    "ws": ("dram", [8, 128, 1], F32), "wr": ("dram", [8, 128, 1], F32),
+    "tab": ("sbuf", [128, 4112], BF),
+    "BI": ("sbuf", [128, 512], I32), "BA": ("sbuf", [128, 512], F32), "BB": ("sbuf", [128, 512], F32), "BT": ("sbuf", [128, 512], F32),
+    "PI": ("sbuf", [8, 128], I32), "PB": ("sbuf", [8, 128], F32), "PC": ("sbuf", [8, 128], F32),
+    "Y": ("sbuf", [128, 512], F32), "VY": ("sbuf", [128, 512], F32), "PO": ("sbuf", [128, 128], F32),
+    "OB": ("sbuf", [128, 512], BF), "OFm": ("sbuf", [128, 256], F32),
+    "IDf": ("sbuf", [128, 256], F32), "IDb": ("sbuf", [128, 256], BF), "IDa": ("sbuf", [128, 256], F16), "IDp": ("sbuf", [128, 256], F16),
+    "IDh": ("sbuf", [128, 128], F16), "BOh": ("sbuf", [128, 128], F16), "Fh": ("sbuf", [128, 128], F16), "ID2": ("sbuf", [128, 256], F32),
+    "REV": ("sbuf", [128, 128], F32), "BOb": ("sbuf", [128, 256], BF), "BO4": ("sbuf", [128, 256], BF), "BOf": ("sbuf", [128, 256], F32),
+    "CK": ("sbuf", [128, 768], BF), "CKm": ("sbuf", [128, 768], BF), "CKa": ("sbuf", [128, 768], BF),
+    "SD": ("sbuf", [128, 2048], BF), "NEG": ("sbuf", [128, 256], BF), "Wq": ("sbuf", [128, 1024], BF),
+    "PW": ("sbuf", [128, 128], F32), "HF": ("sbuf", [128, 128], F32), "ZF": ("sbuf", [128, 128], F32),
+    "SM": ("sbuf", [128, 88], F32), "SI": ("sbuf", [128, 16], I32), "MJ": ("sbuf", [128, 384], F16), "DK": ("sbuf", [128, 16], F32),
+    "AD": ("sbuf", [128, 16], F16), "LX": ("sbuf", [128, 48], F32), "IOK": ("sbuf", [128, 128], BF), "I16": ("sbuf", [128, 384], BF), "ML": ("sbuf", [128, 384], F32),
+    "CS": ("sbuf", [128, 24], F16), "DL": ("sbuf", [128, 24], F16), "RI": ("sbuf", [128, 128], BF),
+    "CR": ("sbuf", [128, 1408], BF), "DM": ("sbuf", [128, 128], F16), "DS": ("sbuf", [128, 128], F32),
+    "MUS": ("sbuf", [128, 512], F32), "A3S": ("sbuf", [128, 512], F32), "RM": ("sbuf", [128, 2048], BF), "S8": ("sbuf", [128, 128], F32),
+    "G": ("sbuf", [128, 8192], BF), "Z": ("sbuf", [128, 8192], BF), "SVs": ("sbuf", [128, 384], F32),
+    "HB": ("sbuf", [128, 128], BF), "MB": ("sbuf", [128, 128], BF), "DT": ("sbuf", [128, 128], F32), "RZ": ("sbuf", [128, 128], BF),
+    "NI": ("sbuf", [128, 128], BF), "tabH": ("sbuf", [128, 4112], BF), "BH": ("sbuf", [128, 512], I32), "HC": ("sbuf", [128, 512], F32),
+    "VH": ("sbuf", [128, 512], F32), "V8": ("sbuf", [8, 512], F32), "vhs": ("dram", [8, 128, 4], F32), "vhr": ("dram", [8, 128, 4], F32),
+    "kS": ("sbuf", [128, 128], I32), "kT": ("sbuf", [128, 128], I32), "kU": ("sbuf", [128, 128], I32), "kL": ("sbuf", [128, 128], BF),
+    "KM": ("sbuf", [128, 384], F16), "KTs": ("sbuf", [128, 24], BF), "LK": ("sbuf", [128, 96], U16), "EH": ("sbuf", [128, 3072], BF),
+    "R": ("sbuf", [128, 1152], F32), "NF": ("sbuf", [128, 384], BF), "IN": ("sbuf", [128, 384], BF), "HS": ("sbuf", [128, 384], F16), "KB": ("sbuf", [128, 384], F32),
+    "WB": ("sbuf", [128, 384], BF), "WK": ("sbuf", [128, 384], BF), "LW": ("sbuf", [128, 48], U16), "TM": ("sbuf", [128, 512], F32),
+    "H1": ("sbuf", [128, 128], F32), "HD": ("sbuf", [128, 128], F32),
+}
+for _k in range(4):
+    SCRATCH["F%d" % _k] = ("sbuf", [128, 640], F32)
+    SCRATCH["E%d" % _k] = ("sbuf", [128, 640], F32)
+SMALL = dict([(_n, ("SM", 8 * _k)) for _k, _n in enumerate(["WC", "DLi", "XF", "IC", "Z0", "Z1", "S1", "S2", "S3", "IW"])] + [("PX", ("SI", 0)), ("XI", ("SI", 8))])
+for _n, _d in (("SX", F32), ("pi", I32), ("pj", I32), ("pk", I32), ("pl", I32), ("of", U16)):
+    SCRATCH[_n] = ("sbuf", [128, 512], _d)
+for _k in range(5):
+    SCRATCH["P%d" % _k] = ("sbuf", [128, 128], F16)
+for _k in range(8):
+    SCRATCH["b%d" % _k] = ("psum", [128, 512], F32)
+SEMAPHORES = (["ah", "ev", "es", "ep", "eg", "ab", "aq", "ay", "aw", "av", "ls"] + ["ax%d" % k for k in range(8)] + ["hx%d" % k for k in range(3)]
+              + ["m%d" % k for k in range(16)] + ["d%d" % k for k in range(26)])
+ESEM = {"v": "ev", "s": "es", "pe": "ep", "g": "eg"}
+CYC = 0.00095
+BONUS = {31:-92,130:186,10:-221,81:-12,120:-237,91:39,126:-53,152:166,46:123,153:107,77:-73,9:279,59:56,151:37,132:-79,88:77,11:253,158:46,37:-79,18:123,116:141,125:-81,54:328,60:-53,53:-54,52:151,44:220,14:39,144:67,131:186,138:-125,157:-161,19:52,56:-57,42:-40,136:229,20:-45,82:199,34:-1,162:-178,69:326,140:28,45:107,47:134,159:24,150:61,133:-162,121:-15,117:-4,63:86,161:-12,78:-30,3:273,109:21,64:-273,26:87,68:-49,66:-226,41:-101,55:256,2:-150,4:-30,50:-94,6:126,105:100,143:57,113:-10,102:-81,110:-26,36:53,149:23,135:-159,119:-184,7:88,13:41,96:30,129:32,21:137,70:153,62:160,155:121,103:25,29:-12,57:131,98:-47,17:90,107:-168,137:-121,93:21,94:-141,39:50,148:72,33:-206,12:-96,23:95,86:-29,111:246,72:-21,25:-132,1:-163,115:122,22:113,71:11,84:-249,35:-102,160:89,142:32,74:77,65:141,118:79,83:-114,43:-32,97:101,92:51,99:-133,141:85,76:91,122:-5,106:34,79:-81,15:66,85:54,89:-50,32:65,51:142,147:14,139:-77,48:-78,49:-3,38:70,87:112,145:-77,27:24,40:-2,134:-105,100:120,128:16,90:-16,67:-46,28:13,8:-112,127:80,101:32,123:68,156:31,114:-70,58:-101,30:75,108:-2,95:-63,146:34,24:7,154:30,61:-74,75:-2,112:-43,104:7,16:-87,73:6,124:5,80:-1,5:4}
+WHERE = "ssvvssssssvssvvs"
+
+
+def R(name, c0, c1, step=1, p0=0, p1=128):
+    if name in SMALL:
+        name, o = SMALL[name]
+        c0, c1 = c0 + o, c1 + o
+    return (name, c0, c1, step, p0, p1)
+
+
+def sub(r, a, b):
+    return (r[0], r[1] + a, r[2] + b, r[3], r[4], r[5])
+
+
+def ncols(r):
+    return (r[2] - r[1] + r[3] - 1) // r[3]
+
+
+def two(r):
+    return SCRATCH[r[0]][2] in (BF, U16, F16)
+
+
+def psum(r):
+    return SCRATCH[r[0]][0] == "psum"
+
+
+def meet(a, b):
+    if a[1] >= b[2] or b[1] >= a[2] or a[4] >= b[5] or b[4] >= a[5]:
+        return False
+    return not (a[3] == b[3] and a[3] > 1 and (a[1] - b[1]) % a[3])
+
+
+def op(L, eng, cost, reads, writes, emit, sem=None, ext=None, rel=0.0, n=1):
+    L.append({"eng": eng, "cost": cost, "r": reads, "w": writes, "emit": emit, "sem": sem, "ext": ext or [], "rel": rel, "n": n})
+    return len(L) - 1
+
+
+def refs(*xs):
+    return [x for x in xs if isinstance(x, tuple)]
+
+
+def tt(L, out, a, b, o):
+    k = 1 if psum(a) or psum(b) else 2
+    return op(L, "v", max(64, ncols(out) * k) * CYC, [a, b], [out],
+              lambda Q, A: [Q["v"].tensor_tensor(out=A(out), in0=A(a), in1=A(b), op=o)])
+
+
+def ts(L, out, a, s1, s2, o0, o1=None):
+    k = 0.5 if two(out) and two(a) else 1
+
+    def emit(Q, A):
+        kw = {} if o1 is None else {"op1": o1}
+        return [Q["v"].tensor_scalar(out=A(out), in0=A(a), scalar1=A(s1) if isinstance(s1, tuple) else s1,
+                                     scalar2=A(s2) if isinstance(s2, tuple) else s2, op0=o0, **kw)]
+    return op(L, "v", max(64, ncols(out) * k) * CYC, [a] + refs(s1, s2), [out], emit)
+
+
+def cp(L, out, a):
+    k = 0.5 if two(out) and two(a) else 1
+    return op(L, "v", max(64, ncols(out) * k) * CYC, [a], [out], lambda Q, A: [Q["v"].tensor_copy(out=A(out), in_=A(a))])
+
+
+def act(L, out, a, bias=0.0):
+    return op(L, "s", max(64, ncols(out)) * CYC + 0.05, [a], [out],
+              lambda Q, A: [Q["s"].activation(out=A(out), in_=A(a), func=ActivationFunctionType.Identity, bias=bias, scale=1.0)])
+
+
+def fill(L, out, c):
+    return op(L, "v", max(64, ncols(out)) * CYC, [], [out], lambda Q, A: [Q["v"].memset(A(out), c)])
+
+
+def mm(L, out, pairs):
+    c = 0.05
+    rd = []
+    for l, r in pairs:
+        c += max(64, ncols(r)) * 0.0006 * (1 if two(l) else 4)
+        rd += [l, r]
+
+    def emit(Q, A):
+        z = None
+        for k in range(len(pairs)):
+            z = Q["pe"].matmul(A(out), A(pairs[k][0]), A(pairs[k][1]), k == 0, k == len(pairs) - 1)
+        return [z]
+    return op(L, "pe", c, rd, [out], emit)
+
+
+def gather(L, out, win, off, eng):
+    def emit(Q, A):
+        if Q["who"][0] == "v":
+            return [Q["v"].tensor_copy(out=A(out), in_=A(win).indirect(A(off)))]
+        return [Q["s"].activation(out=A(out), in_=A(win).indirect(A(off)), func=ActivationFunctionType.Identity, bias=0.0, scale=1.0)]
+    return op(L, eng, 0.06 + ncols(out) * 1.56 * CYC, [win, off], [out], emit)
+
+
+def mms(L, out, pairs):
+    w = ncols(out) // len(pairs)
+    return op(L, "pe", 0.05 + 64 * len(pairs) * 0.0006, [x for p in pairs for x in p], [out],
+              lambda Q, A: [Q["pe"].matmul(A(sub(out, w * k, w * k + w - ncols(out))), A(p[0]), A(p[1]), True, True) for k, p in enumerate(pairs)], n=len(pairs))
+
+
+def asel(L, out, a, pattern, cmp, fillv, base, cm):
+    return op(L, "g", 0.2 + ncols(out) * 2 * CYC, [a], [out],
+              lambda Q, A: [Q["g"].affine_select(A(out), A(a), pattern, cmp, fillv, base, cm)])
+
+
+def iota(L, out, pattern, base, cm):
+    def emit(Q, A):
+        if SCRATCH[out[0]][2] == I32:
+            return [Q["g"].iota(A(out), pattern, base, cm)]
+        return [Q["g"].iota(A(out), pattern, base, cm, allow_small_or_imprecise_dtypes=True)]
+    return op(L, "g", 0.15 + ncols(out) * 2 * CYC, [], [out], emit)
+
+
+def depend(L):
+    hist = {}
+    for i, o in enumerate(L):
+        pred = {}
+        for w, rs in ((False, o["r"]), (True, o["w"])):
+            for x in rs:
+                keep = []
+                for (j, y, yw) in hist.get(x[0], []):
+                    if j == i:
+                        keep.append((j, y, yw))
+                        continue
+                    same = L[j]["eng"] == o["eng"]
+                    hit = (w or yw) and meet(x, y)
+                    if psum(x) and not same:
+                        hit = True
+                    if hit:
+                        pred[j] = True
+                    if not (w and y[1] >= x[1] and y[2] <= x[2] and y[4] >= x[4] and y[5] <= x[5] and x[3] == 1 and not psum(x)):
+                        keep.append((j, y, yw))
+                hist[x[0]] = keep
+        for w, rs in ((False, o["r"]), (True, o["w"])):
+            for x in rs:
+                hist.setdefault(x[0], []).append((i, x, w))
+        o["pred"] = pred
+
+
+def schedule(L, marks, hop=0.12, bonus=None, where=None):
+    bonus = BONUS if bonus is None else bonus
+    where = WHERE if where is None else where
+    n = len(L)
+    k = 0
+    for o in L:
+        if o["eng"] == "vs":
+            o["eng"] = where[k if k < 8 else 8 + (k - 8) % 8]
+            k += 1
+    succ = [[] for _ in range(n)]
+    prio = [0.0] * n
+    left = [len(o["pred"]) for o in L]
+    for i, o in enumerate(L):
+        for j in o["pred"]:
+            succ[j].append(i)
+    for i in range(n - 1, -1, -1):
+        prio[i] = L[i]["cost"] + max([prio[k] + hop for k in succ[i]] + [0.0])
+    for a, b in zip(marks, marks[1:]):
+        for i in range(a, b):
+            prio[i] += bonus.get(b - i, 0)
+    free = {"v": 0.0, "s": 0.0, "pe": 0.0, "g": 5.0, "sy": 0.0, "ss": 0.0}
+    at = [o["rel"] for o in L]
+    ready = [i for i in range(n) if left[i] == 0]
+    order = []
+    busy = dict((k, 0.0) for k in free)
+    while ready:
+        best = None
+        for i in ready:
+            e = L[i]["eng"]
+            key = (max(free[e], at[i]), -prio[i])
+            if best is None or key < best[0]:
+                best = (key, i, e)
+        (t0, _p), i, e = best
+        ready.remove(i)
+        o = L[i]
+        o["eng"] = e
+        o["t0"] = t0
+        fin = t0 + o["cost"]
+        free[e] = fin if e in ESEM else t0 + 0.1
+        busy[e] += o["cost"]
+        o["t1"] = fin
+        order.append(i)
+        for k in succ[i]:
+            at[k] = max(at[k], fin + hop)
+            left[k] -= 1
+            if left[k] == 0:
+                ready.append(k)
+    return order, busy
+
+
+def emit_all(L, order, Q, A, T, tot):
+    known = dict((e, {}) for e in ("v", "s", "pe", "g", "sy", "ss"))
+    for i in order:
+        o = L[i]
+        e = o["eng"]
+        q = Q[e]
+        kn = known[e]
+        need = {}
+        for j in o["pred"]:
+            p = L[j]
+            same = p["eng"] == e and e in ESEM
+            if same and not o["pred"][j]:
+                continue
+            if need.get(p["sem"], (0, None))[0] < p["val"]:
+                need[p["sem"]] = (p["val"], j)
+        for s in sorted(need, key=lambda z: -L[need[z][1]]["t1"]):
+            v, j = need[s]
+            if kn.get(s, 0) >= v:
+                continue
+            q.wait_ge(T.sem[s], v)
+            for s2, v2 in L[j]["clock"].items():
+                if kn.get(s2, 0) < v2:
+                    kn[s2] = v2
+        for s, v in o["ext"]:
+            q.wait_ge(T.sem[s], v)
+        Q["who"][0] = e
+        zs = o["emit"](Q, A)
+        if e in ESEM:
+            s = ESEM[e]
+            for z in zs:
+                z.then_inc(T.sem[s], 1)
+            tot[s] = tot.get(s, 0) + len(zs)
+        else:
+            s = o["sem"]
+            zs[0].then_inc(T.sem[s], 16)
+            tot[s] = 16
+        o["sem"] = s
+        o["val"] = tot[s]
+        ck = dict(kn)
+        ck[s] = tot[s]
+        o["clock"] = ck
+    return known
+
+
+def constants(L):
+    al = AluOpType
+    fill(L, R("OB", 0, 512), 1.0)
+    fill(L, R("OFm", 0, 256), 1.0)
+    fb, ff = R("OB", 0, 256), R("OFm", 0, 256)
+    fill(L, R("tab", 4096, 4112), 0.0)
+    fill(L, R("tabH", 4096, 4112), 0.0)
+    for k in range(4):
+        fill(L, R("F%d" % k, 0, 640), 0.0)
+        fill(L, R("E%d" % k, 0, 640), 0.0)
+    asel(L, R("IDf", 0, 256), ff, [[0, 2], [-1, 128]], al.is_equal, 0.0, 0, 1)
+    asel(L, R("REV", 0, 128), R("OFm", 0, 128), [[-16, 8], [1, 16]], al.is_equal, 0.0, -15, 1)
+    asel(L, R("S8", 0, 128), R("OFm", 0, 128), [[-1, 8], [0, 16]], al.is_equal, 0.0, 0, 1)
+    for m in range(3):
+        asel(L, R("CK", 256 * m, 256 * m + 256), fb, [[0, 2], [-16, 8], [0, 16]], al.is_equal, 0.0, -(15 - m), 1)
+    asel(L, R("BOb", 0, 256), fb, [[0, 2], [-16, 8], [0, 16]], al.is_ge, 0.0, 0, 1)
+    asel(L, R("BOb", 0, 256), R("BOb", 0, 256), [[0, 2], [16, 8], [0, 16]], al.is_ge, 0.0, 15, -1)
+    iota(L, R("MUS", 0, 512), [[8, 4], [32, 128]], 5, 0)
+    iota(L, R("A3S", 0, 512), [[37, 4], [148, 128]], 0, 0)
+    iota(L, R("IOK", 0, 128), [[1, 128]], 0, 0)
+    iota(L, R("PX", 0, 1), [[1, 1]], 0, 1)
+    asel(L, R("I16", 0, 384), R("OB", 0, 384), [[0, 24], [-1, 16]], al.is_equal, 0.0, 0, 1)
+    iota(L, R("DLi", 0, 8), [[16, 8]], 0, 0)
+    fill(L, R("RI", 0, 128), -256.0)
+    iota(L, R("RI", 0, 128, 1, 0, 1), [[-1, 128]], 0, 0)
+    asel(L, R("DS", 0, 128), R("OFm", 0, 128), [[-1, 128]], al.is_equal, 0.0, -1, 1)
+    cp(L, R("IDb", 0, 256), R("IDf", 0, 256))
+    cp(L, R("BOf", 0, 256), R("BOb", 0, 256))
+    ts(L, R("BO4", 0, 256), R("BOb", 0, 256), 4.0, None, al.mult)
+    cp(L, R("ID2", 0, 256), R("IDf", 0, 256))
+    fill(L, R("ID2", 0, 256, 16), 0.0)
+    cp(L, R("IDa", 0, 256), R("ID2", 0, 256))
+    tt(L, R("IDp", 0, 256), R("IDf", 0, 256), R("ID2", 0, 256), al.subtract)
+    cp(L, R("IDh", 0, 128), R("IDf", 0, 128))
+    cp(L, R("BOh", 0, 128), R("BOb", 0, 128))
+    ts(L, R("CKm", 0, 768), R("CK", 0, 768), 32.0, None, al.mult)
+    ts(L, R("CKa", 0, 768), R("CK", 0, 768), 148.0, None, al.mult)
+    fill(L, R("SD", 0, 2048), 0.0)
+    for x in range(16):
+        cp(L, R("SD", 128 * x + x, 128 * x + 128, 16), R("BOb", 0, 128, 16))
+    ts(L, R("NEG", 0, 256), R("IDf", 0, 256), -128.0, None, al.mult)
+    fill(L, R("HF", 0, 128), 0.5)
+    fill(L, R("ZF", 0, 128), 0.0)
+    op(L, "v", 0.12, [R("HF", 0, 128), R("ZF", 0, 128)], [R("PW", 0, 128)],
+       lambda Q, A: [Q["v"].tensor_tensor_scan(out=A(R("PW", 0, 128)), data0=A(R("HF", 0, 128)), data1=A(R("ZF", 0, 128)),
+                                               initial=float(2.0 ** 64), op0=al.mult, op1=al.add)])
+    ts(L, R("b2", 256, 384), R("PW", 0, 128), 2.5, None, al.mult)
+    mm(L, R("b7", 0, 2), [(R("PW", 0, 128, 1, 0, 1), R("OFm", 0, 2, 1, 0, 1))])
+    cp(L, R("WC", 0, 2), R("b7", 0, 2))
+    fill(L, R("Wq", 0, 1024), 0.0)
+    for q in range(8):
+        ts(L, R("Wq", 144 * q, 144 * q + 16), R("OB", 0, 16), R("WC", 0, 1), None, al.mult)
+    mm(L, R("b7", 0, 384), [(R("I16", 0, 128), R("I16", 0, 384))])
+    cp(L, R("ML", 0, 384), R("b7", 0, 384))
+    for k in range(3):
+        cp(L, R("CS", 8 * k, 8 * k + 8), R("BOf", 0, 128, 16))
+    ts(L, R("XI", 0, 1), R("PX", 0, 1), 15, None, al.bitwise_and)
+    cp(L, R("XF", 0, 1), R("XI", 0, 1))
+    ts(L, R("IC", 0, 1), R("PX", 0, 1), 256.0, None, al.add)
+    ts(L, R("IW", 0, 1), R("PX", 0, 1), 128.0, 2.0, al.add, al.mult)
+    ts(L, R("DK", 0, 8), R("DLi", 0, 8), R("XF", 0, 1), None, al.add)
+    ts(L, R("DK", 8, 16), R("DLi", 0, 8), R("XF", 0, 1), 128.0, al.add, al.add)
+    fill(L, R("Z1", 0, 8), 0.0)
+    cp(L, R("AD", 0, 8), R("Z1", 0, 8))
+    ts(L, R("AD", 8, 16), R("Z1", 0, 8), 1.0, None, al.add)
+    for k, b in ((0, 256.0), (1, 384.0), (2, 768.0)):
+        ts(L, R("DL", 8 * k, 8 * k + 8), R("DLi", 0, 8), R("XF", 0, 1), b, al.add, al.add)
+    asel(L, R("DT", 0, 128), R("OFm", 0, 128), [[-1, 128]], al.is_equal, 0.0, 1, 1)
+    fill(L, R("DT", 0, 128, 16), 0.0)
+    tt(L, R("HB", 0, 128), R("IDf", 0, 128), R("DT", 0, 128), al.subtract)
+    ts(L, R("MB", 0, 128), R("DT", 0, 128), -8192.0, None, al.mult)
+    ts(L, R("NI", 0, 128), R("IDf", 0, 128), -1.0, None, al.mult)
+    fill(L, R("RZ", 0, 128, 1, 0, 2), -1.0)
+    fill(L, R("RZ", 0, 128, 1, 0, 1), 7936.0)
+    ts(L, R("Z0", 0, 1), R("XF", 0, 1), 0.0, None, al.is_equal)
+    ts(L, R("S1", 0, 1), R("Z0", 0, 1), -2.0, 1.0, al.mult, al.add)
+    ts(L, R("S3", 0, 1), R("XF", 0, 1), -4.0, 68.0, al.mult, al.add)
+    ts(L, R("Z1", 0, 1), R("Z0", 0, 1), -76.0, None, al.mult)
+    tt(L, R("S2", 0, 1), R("S3", 0, 1), R("Z1", 0, 1), al.add)
+    for k in range(4):
+        fill(L, R("CR", 128 * k, 128 * k + 128), float(8 * k + 5))
+        fill(L, R("CR", 512 + 128 * k, 640 + 128 * k), float(37 * k))
+    for m in range(3):
+        fill(L, R("CR", 1024 + 128 * m, 1152 + 128 * m), float(3 - m))
+    fill(L, R("DS", 0, 128, 16), 0.0)
+    fill(L, R("DS", 15, 128, 16), 0.0)
+    tt(L, R("DM", 0, 128), R("IDf", 0, 128), R("DS", 0, 128), al.subtract)
+    fill(L, R("RM", 0, 2048), 1.0)
+    fill(L, R("RM", 0, 2048, 16), 0.0)
+
+
+def offsets(L, k, src, mul, add):
+    al = AluOpType
+    a = lambda nm: R(nm, 128 * k, 128 * k + 128)
+    tt(L, a("pi"), src, mul, al.mult)
+    ts(L, a("pj"), a("pi"), 5, None, al.arith_shift_right)
+    tt(L, a("pk"), a("pj"), add, al.add)
+    ts(L, a("pl"), a("pk"), MASK, None, al.bitwise_and)
+    ts(L, a("of"), a("pl"), 4096.0, None, al.min)
+
+
+def look(L, k, win="tab"):
+    al = AluOpType
+    for h in range(2):
+        a, b = 1024 * h, 1024 * h + 1024
+        g, z = R("G", 2048 * k + a, 2048 * k + b), R("Z", 2048 * k + a, 2048 * k + b)
+        gather(L, g, R(win, 0, 4112), R("of", 128 * k + 64 * h, 128 * k + 64 * h + 64), "vs")
+
+        def emit(Q, A, g=g, z=z):
+            return [Q["v"].tensor_tensor_scan(out=A(z), data0=A(R("RM", 0, 1024)), data1=A(g), initial=0.0, op0=al.mult, op1=al.max)]
+        op(L, "v", 512 * CYC, [R("RM", 0, 1024), g], [z], emit)
+
+
+def own_value(L, c, k, src, bank, out, win):
+    offsets(L, k, src, R("MUS", 128 * c, 128 * c + 128), R("A3S", 128 * c, 128 * c + 128))
+    look(L, k, win)
+    mm(L, bank, [(R("BOb", 0, 128), R("Z", 2048 * k + 15, 2048 * k + 2048, 16))])
+    act(L, out, bank)
+
+
+def program(r, arrive):
+    al = AluOpType
+    L = []
+    constants(L)
+    gd = lambda q, out, in_, reads, writes, sem, ext, rel: op(
+        L, q, 2.2, reads, writes, lambda Q, A: [Q[q].dma_start(out(A), in_(A))], sem=sem, ext=ext, rel=rel)
+    gd("sy", lambda A: A(R("BI", 0, 512)), lambda A: A("br"), [], [R("BI", 0, 512)], "d0", [("ab", arrive["ab"]), ("m9", 16)], 9.0)
+    gd("sy", lambda A: A(R("PI", 0, 128, 1, 0, 8)), lambda A: A("qr")[:, 16 * r:16 * r + 16, :], [], [R("PI", 0, 128, 1, 0, 8)], "d1",
+       [("aq", arrive["aq"]), ("m10", 16)], 9.0)
+    gd("ss", lambda A: A(R("tab", 0, 4096, 1, 16 * r, 16 * r + 16)), lambda A: A("sight")[16 * r:16 * r + 16, :], [],
+       [R("tab", 0, 4096, 1, 16 * r, 16 * r + 16)], "d2", [], 2.0)
+    for n, (s, cnt) in enumerate(arrive["x"]):
+        gd("sy", lambda A, s=s: A(R("tab", 0, 4096, 1, 16 * s, 16 * s + 16)), lambda A, s=s: A("xr")[s], [],
+           [R("tab", 0, 4096, 1, 16 * s, 16 * s + 16)], "d%d" % (3 + n), [("ax%d" % s, cnt)], 10.0 + n)
+    gd("sy", lambda A: A(R("BH", 0, 512)), lambda A: A("bun"), [], [R("BH", 0, 512)], "d21", [], 1.0)
+    gd("ss", lambda A: A(R("tabH", 0, 4096)), lambda A: A("sight"), [], [R("tabH", 0, 4096)], "d22", [], 3.0)
+    ts(L, R("BB", 0, 512), R("BH", 0, 512), 0.0, 1.0 - OFF, al.is_lt, al.mult)
+    tt(L, R("HC", 0, 512), R("BH", 0, 512), R("BB", 0, 512), al.add)
+    for c in range(4):
+        own_value(L, c, c, R("HC", c, 512, 4), R("b%d" % c, 0, 128), R("VH", 128 * c, 128 * c + 128), "tabH")
+    gd("ss", lambda A: A("vhs"), lambda A: A(R("VH", 0, 512))[0:128:16, :], [R("VH", 0, 512)], [R("vhs", 0, 1)], "d23", [], 0.0)
+    gd("ss", lambda A: A("vhr")[r], lambda A: A(R("VH", 0, 512, 1, 16 * r, 16 * r + 1)), [R("VH", 0, 512)], [R("vhr", 0, 1)], "d24", [], 0.0)
+    op(L, "g", 1.5, [R("vhs", 0, 1)], [R("vhs", 1, 2)], lambda Q, A: Q["values"]())
+    gd("sy", lambda A: A(R("V8", 0, 512, 1, 0, 8)), lambda A: A("vhr"), [R("vhr", 0, 1), R("vhs", 1, 2)], [R("V8", 0, 512, 1, 0, 8)], "d25",
+       [("ah", N - 1)], 0.0)
+    for c in range(4):
+        mm(L, R("b%d" % (4 + c), 128, 256), [(R("S8", 0, 128, 1, 0, 8), R("V8", 128 * c, 128 * c + 128, 1, 0, 8))])
+        act(L, R("F%d" % c, 128, 256), R("b%d" % (4 + c), 128, 256))
+    ts(L, R("BA", 0, 512), R("BI", 0, 512), 0.0, 1.0 - OFF, al.is_lt, al.mult)
+    tt(L, R("BT", 0, 512), R("BI", 0, 512), R("BA", 0, 512), al.add)
+    for c in range(4):
+        mm(L, R("b%d" % (4 + c), 0, 128), [(R("REV", 0, 128), R("BT", c, 512, 4))])
+        act(L, R("F%d" % c, 0, 128), R("b%d" % (4 + c), 0, 128))
+    p8 = lambda nm: R(nm, 0, 128, 1, 0, 8)
+    ts(L, p8("PB"), p8("PI"), 0.0, 1.0 - OFF, al.is_lt, al.mult)
+    tt(L, p8("PC"), p8("PI"), p8("PB"), al.add)
+    mm(L, R("b3", 0, 128), [(p8("S8"), p8("PC"))])
+    ts(L, R("P0", 0, 128), R("b3", 0, 128), -SH, None, al.add)
+    marks = []
+    tile = ["F%d" % c for c in range(4)]
+    for t in range(4):
+        marks.append(len(L))
+        F = tile[t]
+        FB, FV = R(F, 0, 128), R(F, 128, 256)
+        cl = [(t + 1 + m) % 4 for m in range(3)]
+        dl = [0, 1 + t, 2 + t]
+        fwd = lambda nm, m: R(nm, 128 - 16 * dl[m], 256 - 16 * dl[m])
+        bwd = lambda nm, m: R(nm, 16 * dl[m], 16 * dl[m] + 128)
+        ckf = lambda nm, w, m: R(nm, 256 * w + 128 - 16 * dl[m], 256 * w + 256 - 16 * dl[m])
+        bk = lambda b, m: R("b%d" % b, 128 * m, 128 * m + 128)
+        at = lambda nm, m, w=128: R(nm, w * m, w * m + w)
+        P = R("P%d" % t, 0, 128)
+        tt(L, R("kS", 0, 128), FB, FV, al.add)
+        if t:
+            ts(L, R("kT", 0, 128), R("kS", 0, 128), float(13 * t), None, al.add)
+        ts(L, R("kU", 0, 128), R("kT" if t else "kS", 0, 128), 127, None, al.bitwise_and)
+        cp(L, R("kL", 0, 128), R("kU", 0, 128))
+        kL = R("kL", 0, 128)
+        row = lambda a: R("CR", a, a + 128, 1, 0, 1)
+        one = R("OB", 0, 128, 1, 0, 1)
+        Fh = R("Fh", 0, 128)
+        ts(L, Fh, FB, -SH, None, al.add)
+        for m in range(3):
+            mm(L, bk(4 + m, 2), [(fwd("IDp", m), P), (fwd("IDa", m), Fh)])
+            sx = at("SX", m)
+            act(L, sx, bk(4 + m, 2), SH)
+            mm(L, bk(1 + m, 0), [(one, row(128 * cl[m])), (ckf("CKm", m, m), kL)])
+            mm(L, bk(1 + m, 1), [(one, row(512 + 128 * cl[m])), (ckf("CKa", m, m), kL)])
+            offsets(L, m, sx, bk(1 + m, 0), bk(1 + m, 1))
+            look(L, m)
+        mm(L, bk(3, 3), [(R("DM", 0, 128), Fh)])
+        for m in range(3):
+            mm(L, bk(0, m), [(R("RI", 0, 128, 1, 0, 2), R("OB", 0, 128, 1, 0, 2)), (kL, ckf("CK", m, m))])
+        op(L, "s", 0.12, [R("b0", 0, 384, 16), R("IC", 0, 1)], [R("KTs", 0, 24)], lambda Q, A: [Q["s"].activation(
+            out=A(R("KTs", 0, 24)), in_=A(R("b0", 0, 384, 16)), func=ActivationFunctionType.Identity, bias=A(R("IC", 0, 1)), scale=1.0)])
+        for m in range(3):
+            tt(L, at("KM", m), bk(0, m), at("ML", m), al.mult)
+            mm(L, R("b0", 384 + 24 * m, 408 + 24 * m), [(at("KM", m), R("CS", 0, 24)), (R("IDh", 0, 128), R("DL", 0, 24))])
+        cp(L, R("LK", 0, 72), R("b0", 384, 456))
+        for m in range(3):
+            for h in range(2):
+                def emit(Q, A, m=m, h=h):
+                    return [Q["v"].tensor_scalar(out=A(R("EH", 1024 * m + 128 * q, 1024 * m + 128 * q + 128)), in0=A(R("IOK", 0, 128)),
+                                                 scalar1=A(R("KTs", 8 * m + q, 8 * m + q + 1)), scalar2=None, op0=al.is_equal)
+                            for q in range(4 * h, 4 * h + 4)]
+                op(L, "v", 4 * 64 * CYC, [R("IOK", 0, 128), R("KTs", 8 * m + 4 * h, 8 * m + 4 * h + 4)],
+                   [R("EH", 1024 * m + 512 * h, 1024 * m + 512 * h + 512)], emit, n=4)
+            mm(L, R("b%d" % (4 + m), 384, 512),
+               [(R("Wq", 128 * q, 128 * q + 128), R("EH", 1024 * m + 128 * q, 1024 * m + 128 * q + 128)) for q in range(8)])
+            Fc = tile[cl[m]]
+            act(L, R(Fc, 512, 640), R("b%d" % (4 + m), 384, 512))
+            gather(L, at("R", m, 384), R(Fc, 0, 640), R("LK", 24 * m, 24 * m + 24), "s")
+            tt(L, at("NF", m), R("R", 384 * m + 256, 384 * m + 384), R("b2", 256, 384), al.is_ge)
+        for m in range(3):
+            sv, mk, nv, hot = [R("b%d" % (4 + m), 128 * k, 128 * k + 128) for k in range(4)]
+            for h in (0, 64):
+                mm(L, sub(sv, h, h - 64), [(R("SD", 128 * x, 128 * x + 128), R("Z", 2048 * m + 16 * h + x, 2048 * m + 16 * h + 1024, 16))
+                                           for x in range(16)])
+            tt(L, at("IN", m), sv, R("R", 384 * m + 128, 384 * m + 256), al.is_gt)
+            mm(L, bk(7, m), [(one, row(1024 + 128 * m)), (bwd("BO4", m), at("IN", m)), (bwd("NEG", m), at("NF", m))])
+            act(L, at("SVs", m), sv, -2040.0)
+            mm(L, mk, [(R("RZ", 0, 128, 1, 0, 2), R("OB", 0, 128, 1, 0, 2)), (R("MB", 0, 128), at("IN", m))])
+            mm(L, hot, [(R("HB", 0, 128), at("IN", m))])
+            tt(L, R(tile[cl[m]], 256, 512, 2), mk, at("SX", m), al.min)
+            tt(L, at("HS", m), hot, at("SVs", m), al.mult)
+            mm(L, nv, [(R("BOh", 0, 128), at("HS", m))])
+            act(L, R(tile[cl[m]], 257, 512, 2), nv, 2040.0)
+        ts(L, at("KB", 0), bk(7, 0), 3.25, None, al.max)
+        tt(L, at("KB", 1), at("KB", 0), bk(7, 1), al.max)
+        tt(L, at("KB", 2), at("KB", 1), bk(7, 2), al.max)
+        kb = at("KB", 2)
+        for m in range(3):
+            tt(L, at("WB", m), kb, bk(7, m), al.is_equal)
+            mm(L, bk(1 + m, 0), [(at("WB", m), ckf("CK", 0, m))])
+            ts(L, at("WK", m), bk(1 + m, 0), R("IW", 0, 1), None, al.mult)
+            mms(L, bk(4 + m, 0), [(R("EH", 1024 * m + 128 * q, 1024 * m + 128 * q + 128), R("WK", 128 * m + 16 * q, 128 * m + 16 * q + 16)) for q in range(8)])
+            tt(L, at("MJ", m), bk(4 + m, 0), at("ML", m), al.mult)
+            b16 = R("b0", 384 + 16 * m, 400 + 16 * m)
+            mm(L, b16, [(at("MJ", m), R("CS", 0, 16)), (R("IDh", 0, 128), R("AD", 0, 16))])
+            tt(L, at("LX", m, 16), b16, R("DK", 0, 16), al.max)
+            cp(L, at("LW", m, 16), at("LX", m, 16))
+            new = tile[cl[m]].replace("F", "e").replace("E", "F").replace("e", "E")
+            gather(L, R(new, 0, 256), R(tile[cl[m]], 0, 512), at("LW", m, 16), "s")
+            tile[cl[m]] = new
+        ts(L, R("H1", 0, 128), kb, R("S1", 0, 1), R("S2", 0, 1), al.mult, al.is_gt)
+        tt(L, R("HD", 0, 128), R("H1", 0, 128), bk(3, 3), al.mult)
+        mm(L, bk(2, 3), [(R("BOf", 112, 240), R("HD", 0, 128))])
+        cp(L, R("P%d" % (t + 1), 0, 128), bk(2, 3))
+        mm(L, bk(1, 2), [(one, R("OB", 0, 128, 1, 0, 1))] + [(R("NI", 0, 128), at("WB", m)) for m in range(3)])
+        tt(L, at("TM", 3), bk(1, 2), at("SX", 0), al.mult)
+        for m in range(3):
+            mm(L, bk(1 + m, 1), [(fwd("IDb", m), at("WB", m))])
+            tt(L, at("TM", m), bk(1 + m, 1), R("R", 384 * m, 384 * m + 128), al.mult)
+        mm(L, bk(3, 2), [(R("IDf", 0, 128), at("TM", 3))] + [(bwd("IDf", m), at("TM", m)) for m in range(3)])
+        act(L, FB, bk(3, 2))
+        own_value(L, t, 3, bk(3, 2), bk(1, 3), FV, "tab")
+    marks.append(len(L))
+    for c in range(4):
+        mm(L, R("b%d" % (4 + c), 0, 128), [(R("REV", 0, 128), R(tile[c], 0, 128))])
+        ts(L, R("Y", c, 512, 4), R("b%d" % (4 + c), 0, 128), -1.0, None, al.max)
+        act(L, R("VY", c, 512, 4), R(tile[c], 128, 256))
+    ts(L, R("PO", 0, 128), R("P4", 0, 128), SH, -1.0, al.add, al.max)
+    e = {}
+    e["y"] = gd("sy", lambda A: A("ys"), lambda A: A(R("Y", 0, 512)), [R("Y", 0, 512)], [], "d12", [], 0.0)
+    e["w"] = gd("sy", lambda A: A("ws"), lambda A: A(R("PO", 0, 128, 1, 0, 128))[0:128:16, :], [R("PO", 0, 128)], [], "d13", [], 0.0)
+    gd("sy", lambda A: A("yr")[r], lambda A: A(R("Y", 0, 512, 1, 16 * r, 16 * r + 16)), [R("Y", 0, 512)], [], "d14", [], 0.0)
+    gd("sy", lambda A: A("wr")[r], lambda A: A(R("PO", 0, 128, 1, 16 * r, 16 * r + 1)), [R("PO", 0, 128)], [], "d15", [], 0.0)
+    e["v"] = gd("sy", lambda A: A("vs"), lambda A: A(R("VY", 0, 512))[0:128:16, :], [R("VY", 0, 512)], [], "d16", [], 0.0)
+    gd("sy", lambda A: A("vr")[r], lambda A: A(R("VY", 0, 512, 1, 16 * r, 16 * r + 1)), [R("VY", 0, 512)], [], "d17", [], 0.0)
+    return L, marks
+
+
+def plan(T, topo):
+    cores = [int(c) for c in T.cores]
+    out = {}
+    for r, c in enumerate(cores):
+        mate = [s for s in range(N) if s != r and topo.chip(cores[s]) == topo.chip(c)]
+        away = [s for s in range(N) if topo.chip(cores[s]) != topo.chip(c)]
+        here = [s for s in range(N) if topo.chip(cores[s]) == topo.chip(c)]
+        cand = [h for h in topo.cores_of(c) if topo.die(h) != topo.die(c) and h not in cores and all(topo.may_write(h, cores[s]) for s in away)]
+        k = here.index(r)
+        chips = sorted(set(topo.chip(cores[s]) for s in away))
+        direct, helped = [], []
+        for ch in chips:
+            two_ = [s for s in away if topo.chip(cores[s]) == ch]
+            direct.append(two_[k % 2])
+            helped.append(two_[(k + 1) % 2])
+        out[r] = {"mate": mate[0], "away": away, "direct": direct, "helped": helped, "helper": cand[k]}
+    return cores, out
+
+
+def bits(es):
+    return sum(1 << int(x) for x in es)
+
+
+def groups(p, r, cores, topo):
+    me = cores[r]
+    off = topo.engines(me, cores[p["away"][0]])
+    on = [x for x in topo.engines(me, cores[p["mate"]]) if x not in off]
+    a = [(s, off[2 * k:2 * k + 2]) for k, s in enumerate(p["away"][:4])] + [(p["mate"], on)]
+    b = [(s, off[4 * k:4 * k + 4]) for k, s in enumerate(p["away"][4:6])]
+    return [a, b], [[(s, off[k:k + 1]) for k, s in enumerate(p["away"])] + [(p["mate"], on[:1])]]
+
+
+def rank_program(g, core, T, topo):
+    cores, pl = plan(T, topo)
+    rank = T.rank_of(core)
+    addr = lambda c: topo.addr(c)[:2]
+
+    def write(dst, o, i, rs, es):
+        rid, pid = addr(dst)
+        g.remote_dma(out_ap=o, in_ap=i, remote_sem=T.sem[rs], local_sem=T.sem["ls"], pid=pid, routing_id=rid, dma_engine_mask=bits(es))
+        return len(es)
+
+    if rank is None:
+        for r in range(N):
+            p = pl[r]
+            if p["helper"] != core:
+                continue
+            n = 0
+            for k, s in enumerate(p["helped"]):
+                es = topo.engines(core, cores[s])
+                g.wait_ge(T.sem["hx%d" % k], 8)
+                n += write(cores[s], T["xr"][r], T["xr"][k], "ax%d" % r, es)
+            g.wait_ge(T.sem["ls"], n)
+        return
+
+    r, p = rank, pl[rank]
+    off = topo.engines(core, cores[p["away"][0]])
+    on = [x for x in topo.engines(core, cores[p["mate"]]) if x not in off]
+    many, single = groups(p, r, cores, topo)
+
+    def cnt(s, d, which):
+        for call in groups(pl[s], s, cores, topo)[which]:
+            for dd, es in call:
+                if dd == d:
+                    return len(es)
+
+    others = [s for s in range(N) if s != r]
+    arrive = {"ab": sum(cnt(s, r, 0) for s in others), "aq": len(others)}
+    first = [s for s in others if s == p["mate"] or r in pl[s]["direct"]]
+    arrive["x"] = [(s, len(on) if s == p["mate"] else 8) for s in first + [s for s in others if s not in first]]
+
+    seq = []
+    for k in range(3):
+        seq += [("h", p["helped"][k], k), ("d", p["direct"][k], k)]
+    seq.append(("m", p["mate"], 0))
+    for n, (kind, s, k) in enumerate(seq):
+        q = (g.sync, g.scalar)[n % 2]
+        q.dma_start(T["xs"][s], T["sight"][16 * s:16 * s + 16, :]).then_inc(T.sem["m%d" % n], 16)
+        if n == 1:
+            g.sync.dma_start(T["bs"][:], T["bun"][:]).then_inc(T.sem["m7"], 16)
+            g.scalar.dma_start(T["qs"][:], T["pots"][:]).then_inc(T.sem["m8"], 16)
+            g.sync.dma_start(T["br"][r], T["bun"][16 * r:16 * r + 16, :]).then_inc(T.sem["m9"], 16)
+            g.scalar.dma_start(T["qr"][r], T["pots"][:]).then_inc(T.sem["m10"], 16)
+    tot = {}
+    loc = [0]
+
+    def fused(calls, src, dst, sem):
+        for call in calls:
+            tr = []
+            for s, es in call:
+                rid, pid = addr(cores[s])
+                tr.append(RemoteDMATransfer(dst_ids=[DstId(rid=rid, pnc=pid)], dma_engine_mask=bits(es), remote_sem=T.sem[sem],
+                                            src=T[src][s], dst=T[dst][r]))
+                loc[0] += len(es)
+            g.remote_dma_fused(tr, local_sem=T.sem["ls"])
+
+    for n, (kind, s, k) in enumerate(seq):
+        g.wait_ge(T.sem["m%d" % n], 16)
+        if kind == "h":
+            loc[0] += write(p["helper"], T["xr"][k], T["xs"][s], "hx%d" % k, on)
+        else:
+            loc[0] += write(cores[s], T["xr"][r], T["xs"][s], "ax%d" % r, off if kind == "d" else on)
+        if n == 1:
+            g.wait_ge(T.sem["m7"], 16)
+            fused(many, "bs", "br", "ab")
+            g.wait_ge(T.sem["m8"], 16)
+            ids, ds = [], []
+            for d in others:
+                rid, pid = addr(cores[d])
+                ids.append(DstId(rid=rid, pnc=pid))
+                ds.append(T["qr"][r])
+            g.remote_dma_fused([RemoteDMATransfer(dst_ids=ids, dma_engine_mask=bits(off[:1]), remote_sem=T.sem["aq"], srcs=[T["qs"][:]], dsts=ds)],
+                               local_sem=T.sem["ls"])
+            loc[0] += 1
+
+    L, marks = program(r, arrive)
+    depend(L)
+    order, busy = schedule(L, marks)
+    def values():
+        fused(single, "vhs", "vhr", "ah")
+        return []
+
+    Q = {"values": values, "v": g.vector, "s": g.scalar, "pe": g.tensor, "g": g, "sy": g.sync, "ss": g.scalar, "who": [None]}
+
+    def A(x):
+        if isinstance(x, str):
+            return T[x][:]
+        nm, c0, c1, st, p0, p1 = x
+        return T[nm][p0:p1, c0:c1] if st == 1 else T[nm][p0:p1, c0:c1:st]
+    emit_all(L, order, Q, A, T, tot)
+
+    g.wait_ge(T.sem["d12"], 16)
+    fused(many, "ys", "yr", "ay")
+    g.wait_ge(T.sem["d13"], 16)
+    fused(single, "ws", "wr", "aw")
+    g.wait_ge(T.sem["d16"], 16)
+    fused(single, "vs", "vr", "av")
+    g.sync.wait_ge(T.sem["d14"], 16)
+    g.sync.wait_ge(T.sem["ay"], arrive["ab"])
+    g.sync.dma_start(T["yb"][:], T["yr"][:]).then_inc(T.sem["d18"], 16)
+    g.sync.wait_ge(T.sem["d15"], 16)
+    g.sync.wait_ge(T.sem["aw"], len(others))
+    g.sync.dma_start(T["yp"][:], T["wr"][:]).then_inc(T.sem["d19"], 16)
+    g.sync.wait_ge(T.sem["d17"], 16)
+    g.sync.wait_ge(T.sem["av"], len(others))
+    g.sync.dma_start(T["yv"][:], T["vr"][:]).then_inc(T.sem["d20"], 16)
+    for s in sorted(tot):
+        g.wait_ge(T.sem[s], tot[s])
+    g.wait_ge(T.sem["ls"], loc[0])
+    for s in ("d18", "d19", "d20"):
+        g.wait_ge(T.sem[s], 16)

@@ -34,7 +34,8 @@ SCRATCH = {
     "G": ("sbuf", [128, 8192], BF), "Z": ("sbuf", [128, 8192], BF), "SVs": ("sbuf", [128, 384], F32),
     "HB": ("sbuf", [128, 128], BF), "MB": ("sbuf", [128, 128], BF), "DT": ("sbuf", [128, 128], F32), "RZ": ("sbuf", [128, 128], BF),
     "NI": ("sbuf", [128, 128], BF), "tabH": ("sbuf", [128, 4112], BF), "BH": ("sbuf", [128, 512], I32), "HC": ("sbuf", [128, 512], F32),
-    "VH": ("sbuf", [128, 512], F32), "V8": ("sbuf", [8, 512], F32), "vhs": ("dram", [8, 128, 4], F32), "vhr": ("dram", [8, 128, 4], F32),
+    "VH": ("sbuf", [128, 512], F32), "V8": ("sbuf", [8, 512], F32), "vhs": ("dram", [8, 128, 3], F32), "vhr": ("dram", [8, 128, 3], F32),
+    "vas": ("dram", [8, 128, 1], F32), "var": ("dram", [8, 128, 1], F32),
     "kS": ("sbuf", [128, 128], I32), "kT": ("sbuf", [128, 128], I32), "kU": ("sbuf", [128, 128], I32), "kL": ("sbuf", [128, 128], BF),
     "KM": ("sbuf", [128, 384], F16), "KTs": ("sbuf", [128, 24], BF), "LK": ("sbuf", [128, 96], U16), "EH": ("sbuf", [128, 3072], BF),
     "R": ("sbuf", [128, 1152], F32), "NF": ("sbuf", [128, 384], BF), "IN": ("sbuf", [128, 384], BF), "HS": ("sbuf", [128, 384], F16), "KB": ("sbuf", [128, 384], F32),
@@ -51,12 +52,12 @@ for _k in range(5):
     SCRATCH["P%d" % _k] = ("sbuf", [128, 128], F16)
 for _k in range(8):
     SCRATCH["b%d" % _k] = ("psum", [128, 512], F32)
-SEMAPHORES = (["ah", "ev", "es", "ep", "eg", "ab", "aq", "ay", "aw", "av", "ls"] + ["ax%d" % k for k in range(8)] + ["hx%d" % k for k in range(3)]
-              + ["m%d" % k for k in range(16)] + ["d%d" % k for k in range(26)])
+SEMAPHORES = (["aa", "ah", "ev", "es", "ep", "eg", "ab", "aq", "ay", "aw", "av", "ls"] + ["ax%d" % k for k in range(8)] + ["hx%d" % k for k in range(3)]
+              + ["m%d" % k for k in range(16)] + ["d%d" % k for k in range(30)])
 ESEM = {"v": "ev", "s": "es", "pe": "ep", "g": "eg"}
 CYC = 0.00095
-BONUS = {31:-92,130:186,10:-221,81:-12,120:-237,91:39,126:-53,152:166,46:123,153:107,77:-73,9:279,59:56,151:37,132:-79,88:77,11:253,158:46,37:-79,18:123,116:141,125:-81,54:328,60:-53,53:-54,52:151,44:220,14:39,144:67,131:186,138:-125,157:-161,19:52,56:-57,42:-40,136:229,20:-45,82:199,34:-1,162:-178,69:326,140:28,45:107,47:134,159:24,150:61,133:-162,121:-15,117:-4,63:86,161:-12,78:-30,3:273,109:21,64:-273,26:87,68:-49,66:-226,41:-101,55:256,2:-150,4:-30,50:-94,6:126,105:100,143:57,113:-10,102:-81,110:-26,36:53,149:23,135:-159,119:-184,7:88,13:41,96:30,129:32,21:137,70:153,62:160,155:121,103:25,29:-12,57:131,98:-47,17:90,107:-168,137:-121,93:21,94:-141,39:50,148:72,33:-206,12:-96,23:95,86:-29,111:246,72:-21,25:-132,1:-163,115:122,22:113,71:11,84:-249,35:-102,160:89,142:32,74:77,65:141,118:79,83:-114,43:-32,97:101,92:51,99:-133,141:85,76:91,122:-5,106:34,79:-81,15:66,85:54,89:-50,32:65,51:142,147:14,139:-77,48:-78,49:-3,38:70,87:112,145:-77,27:24,40:-2,134:-105,100:120,128:16,90:-16,67:-46,28:13,8:-112,127:80,101:32,123:68,156:31,114:-70,58:-101,30:75,108:-2,95:-63,146:34,24:7,154:30,61:-74,75:-2,112:-43,104:7,16:-87,73:6,124:5,80:-1,5:4}
-WHERE = "ssvvssssssvssvvs"
+BONUS = {148:-35,134:-38,27:-55,105:25,25:-30,129:-9,3:-24,146:-24,94:-16,93:-9,131:-35,133:-42,127:-10,154:33,88:-84,35:-43,106:12,155:-7,104:-50,40:-24,2:-25,73:32,29:-28,121:-30,125:-29,144:48,158:28,52:-5,61:-49,128:-7,109:-30,1080:-15,23:22,1077:-2,1143:20,1037:-2,110:20,1026:-5,1027:-8,1173:7,80:-20,1024:5,1012:-20,1150:20,45:18,1107:-5,1160:-2,1152:-5,42:2,1066:-2,1008:-10,1149:2,135:-10,1042:-2,53:2,64:10}
+WHERE = "svsvsvsssssvvssssssvvssv"
 
 
 def R(name, c0, c1, step=1, p0=0, p1=128):
@@ -118,13 +119,13 @@ def cp(L, out, a):
     return op(L, "v", max(64, ncols(out) * k) * CYC, [a], [out], lambda Q, A: [Q["v"].tensor_copy(out=A(out), in_=A(a))])
 
 
-def act(L, out, a, bias=0.0):
+def act(L, out, a, bias=0.0, scale=1.0):
     return op(L, "s", max(64, ncols(out)) * CYC + 0.05, [a], [out],
-              lambda Q, A: [Q["s"].activation(out=A(out), in_=A(a), func=ActivationFunctionType.Identity, bias=bias, scale=1.0)])
+              lambda Q, A: [Q["s"].activation(out=A(out), in_=A(a), func=ActivationFunctionType.Identity, bias=bias, scale=scale)])
 
 
 def fill(L, out, c):
-    return op(L, "v", max(64, ncols(out)) * CYC, [], [out], lambda Q, A: [Q["v"].memset(A(out), c)])
+    return op(L, "v", max(64, ncols(out) * (0.5 if two(out) else 1)) * CYC, [], [out], lambda Q, A: [Q["v"].memset(A(out), c)])
 
 
 def mm(L, out, pairs):
@@ -202,7 +203,7 @@ def schedule(L, marks, hop=0.12, bonus=None, where=None):
     k = 0
     for o in L:
         if o["eng"] == "vs":
-            o["eng"] = where[k if k < 8 else 8 + (k - 8) % 8]
+            o["eng"] = where[k if k < 8 else 8 + (k - 8) % 8 if k < 32 else k - 16]
             k += 1
     succ = [[] for _ in range(n)]
     prio = [0.0] * n
@@ -215,7 +216,9 @@ def schedule(L, marks, hop=0.12, bonus=None, where=None):
     for a, b in zip(marks, marks[1:]):
         for i in range(a, b):
             prio[i] += bonus.get(b - i, 0)
-    free = {"v": 0.0, "s": 0.0, "pe": 0.0, "g": 5.0, "sy": 0.0, "ss": 0.0}
+    for i in range(marks[0]):
+        prio[i] += L[i].get("boost", bonus.get(1000 + i, 0))
+    free = {"v": 0.0, "s": 0.0, "pe": 0.0, "g": 0.0, "sy": 0.0, "ss": 0.0}
     at = [o["rel"] for o in L]
     ready = [i for i in range(n) if left[i] == 0]
     order = []
@@ -279,7 +282,8 @@ def emit_all(L, order, Q, A, T, tot):
             tot[s] = tot.get(s, 0) + len(zs)
         else:
             s = o["sem"]
-            zs[0].then_inc(T.sem[s], 16)
+            for z in zs:
+                z.then_inc(T.sem[s], 16)
             tot[s] = 16
         o["sem"] = s
         o["val"] = tot[s]
@@ -291,14 +295,17 @@ def emit_all(L, order, Q, A, T, tot):
 
 def constants(L):
     al = AluOpType
+    L[iota(L, R("MUS", 0, 512), [[8, 4], [32, 128]], 5, 0)]["boost"] = 3000
+    L[iota(L, R("A3S", 0, 512), [[37, 4], [148, 128]], 0, 0)]["boost"] = 3000
+    L[op(L, "g", 4.5, [R("MUS", 0, 512), R("A3S", 0, 512)], [], lambda Q, A: Q["exchange"]())]["boost"] = 2000
     fill(L, R("OB", 0, 512), 1.0)
     fill(L, R("OFm", 0, 256), 1.0)
     fb, ff = R("OB", 0, 256), R("OFm", 0, 256)
     fill(L, R("tab", 4096, 4112), 0.0)
     fill(L, R("tabH", 4096, 4112), 0.0)
     for k in range(4):
-        fill(L, R("F%d" % k, 0, 640), 0.0)
-        fill(L, R("E%d" % k, 0, 640), 0.0)
+        fill(L, R("F%d" % k, 256, 512), 0.0)
+        fill(L, R("E%d" % k, 256, 512), 0.0)
     asel(L, R("IDf", 0, 256), ff, [[0, 2], [-1, 128]], al.is_equal, 0.0, 0, 1)
     asel(L, R("REV", 0, 128), R("OFm", 0, 128), [[-16, 8], [1, 16]], al.is_equal, 0.0, -15, 1)
     asel(L, R("S8", 0, 128), R("OFm", 0, 128), [[-1, 8], [0, 16]], al.is_equal, 0.0, 0, 1)
@@ -306,8 +313,6 @@ def constants(L):
         asel(L, R("CK", 256 * m, 256 * m + 256), fb, [[0, 2], [-16, 8], [0, 16]], al.is_equal, 0.0, -(15 - m), 1)
     asel(L, R("BOb", 0, 256), fb, [[0, 2], [-16, 8], [0, 16]], al.is_ge, 0.0, 0, 1)
     asel(L, R("BOb", 0, 256), R("BOb", 0, 256), [[0, 2], [16, 8], [0, 16]], al.is_ge, 0.0, 15, -1)
-    iota(L, R("MUS", 0, 512), [[8, 4], [32, 128]], 5, 0)
-    iota(L, R("A3S", 0, 512), [[37, 4], [148, 128]], 0, 0)
     iota(L, R("IOK", 0, 128), [[1, 128]], 0, 0)
     iota(L, R("PX", 0, 1), [[1, 1]], 0, 1)
     asel(L, R("I16", 0, 384), R("OB", 0, 384), [[0, 24], [-1, 16]], al.is_equal, 0.0, 0, 1)
@@ -315,21 +320,21 @@ def constants(L):
     fill(L, R("RI", 0, 128), -256.0)
     iota(L, R("RI", 0, 128, 1, 0, 1), [[-1, 128]], 0, 0)
     asel(L, R("DS", 0, 128), R("OFm", 0, 128), [[-1, 128]], al.is_equal, 0.0, -1, 1)
-    cp(L, R("IDb", 0, 256), R("IDf", 0, 256))
-    cp(L, R("BOf", 0, 256), R("BOb", 0, 256))
-    ts(L, R("BO4", 0, 256), R("BOb", 0, 256), 4.0, None, al.mult)
-    cp(L, R("ID2", 0, 256), R("IDf", 0, 256))
+    act(L, R("IDb", 0, 256), R("IDf", 0, 256))
+    act(L, R("BOf", 0, 256), R("BOb", 0, 256))
+    act(L, R("BO4", 0, 256), R("BOb", 0, 256), 0.0, 4.0)
+    act(L, R("ID2", 0, 256), R("IDf", 0, 256))
     fill(L, R("ID2", 0, 256, 16), 0.0)
     cp(L, R("IDa", 0, 256), R("ID2", 0, 256))
     tt(L, R("IDp", 0, 256), R("IDf", 0, 256), R("ID2", 0, 256), al.subtract)
     cp(L, R("IDh", 0, 128), R("IDf", 0, 128))
     cp(L, R("BOh", 0, 128), R("BOb", 0, 128))
-    ts(L, R("CKm", 0, 768), R("CK", 0, 768), 32.0, None, al.mult)
-    ts(L, R("CKa", 0, 768), R("CK", 0, 768), 148.0, None, al.mult)
+    act(L, R("CKm", 0, 768), R("CK", 0, 768), 0.0, 32.0)
+    act(L, R("CKa", 0, 768), R("CK", 0, 768), 0.0, 148.0)
     fill(L, R("SD", 0, 2048), 0.0)
     for x in range(16):
         cp(L, R("SD", 128 * x + x, 128 * x + 128, 16), R("BOb", 0, 128, 16))
-    ts(L, R("NEG", 0, 256), R("IDf", 0, 256), -128.0, None, al.mult)
+    act(L, R("NEG", 0, 256), R("IDf", 0, 256), 0.0, -128.0)
     fill(L, R("HF", 0, 128), 0.5)
     fill(L, R("ZF", 0, 128), 0.0)
     op(L, "v", 0.12, [R("HF", 0, 128), R("ZF", 0, 128)], [R("PW", 0, 128)],
@@ -359,8 +364,8 @@ def constants(L):
     asel(L, R("DT", 0, 128), R("OFm", 0, 128), [[-1, 128]], al.is_equal, 0.0, 1, 1)
     fill(L, R("DT", 0, 128, 16), 0.0)
     tt(L, R("HB", 0, 128), R("IDf", 0, 128), R("DT", 0, 128), al.subtract)
-    ts(L, R("MB", 0, 128), R("DT", 0, 128), -8192.0, None, al.mult)
-    ts(L, R("NI", 0, 128), R("IDf", 0, 128), -1.0, None, al.mult)
+    act(L, R("MB", 0, 128), R("DT", 0, 128), 0.0, -8192.0)
+    act(L, R("NI", 0, 128), R("IDf", 0, 128), 0.0, -1.0)
     fill(L, R("RZ", 0, 128, 1, 0, 2), -1.0)
     fill(L, R("RZ", 0, 128, 1, 0, 1), 7936.0)
     ts(L, R("Z0", 0, 1), R("XF", 0, 1), 0.0, None, al.is_equal)
@@ -376,8 +381,8 @@ def constants(L):
     fill(L, R("DS", 0, 128, 16), 0.0)
     fill(L, R("DS", 15, 128, 16), 0.0)
     tt(L, R("DM", 0, 128), R("IDf", 0, 128), R("DS", 0, 128), al.subtract)
-    fill(L, R("RM", 0, 2048), 1.0)
-    fill(L, R("RM", 0, 2048, 16), 0.0)
+    fill(L, R("RM", 0, 1024), 1.0)
+    fill(L, R("RM", 0, 1024, 16), 0.0)
 
 
 def offsets(L, k, src, mul, add):
@@ -423,17 +428,23 @@ def program(r, arrive):
     for n, (s, cnt) in enumerate(arrive["x"]):
         gd("sy", lambda A, s=s: A(R("tab", 0, 4096, 1, 16 * s, 16 * s + 16)), lambda A, s=s: A("xr")[s], [],
            [R("tab", 0, 4096, 1, 16 * s, 16 * s + 16)], "d%d" % (3 + n), [("ax%d" % s, cnt)], 10.0 + n)
-    gd("sy", lambda A: A(R("BH", 0, 512)), lambda A: A("bun"), [], [R("BH", 0, 512)], "d21", [], 1.0)
-    gd("ss", lambda A: A(R("tabH", 0, 4096)), lambda A: A("sight"), [], [R("tabH", 0, 4096)], "d22", [], 3.0)
+    op(L, "sy", 3.5, [], [R("BH", 0, 512)], lambda Q, A: [], sem="d21")
+    op(L, "ss", 6.0, [], [R("tabH", 0, 4096)], lambda Q, A: [], sem="d22")
     ts(L, R("BB", 0, 512), R("BH", 0, 512), 0.0, 1.0 - OFF, al.is_lt, al.mult)
     tt(L, R("HC", 0, 512), R("BH", 0, 512), R("BB", 0, 512), al.add)
     for c in range(4):
         own_value(L, c, c, R("HC", c, 512, 4), R("b%d" % c, 0, 128), R("VH", 128 * c, 128 * c + 128), "tabH")
-    gd("ss", lambda A: A("vhs"), lambda A: A(R("VH", 0, 512))[0:128:16, :], [R("VH", 0, 512)], [R("vhs", 0, 1)], "d23", [], 0.0)
-    gd("ss", lambda A: A("vhr")[r], lambda A: A(R("VH", 0, 512, 1, 16 * r, 16 * r + 1)), [R("VH", 0, 512)], [R("vhr", 0, 1)], "d24", [], 0.0)
-    op(L, "g", 1.5, [R("vhs", 0, 1)], [R("vhs", 1, 2)], lambda Q, A: Q["values"]())
-    gd("sy", lambda A: A(R("V8", 0, 512, 1, 0, 8)), lambda A: A("vhr"), [R("vhr", 0, 1), R("vhs", 1, 2)], [R("V8", 0, 512, 1, 0, 8)], "d25",
-       [("ah", N - 1)], 0.0)
+        if c in (0, 3):
+            a, b = (0, 128) if c == 0 else (128, 512)
+            x, y, z = ("vas", "var", "aa") if c == 0 else ("vhs", "vhr", "ah")
+            k = 23 if c == 0 else 26
+            gd("ss", lambda A, x=x, a=a, b=b: A(x), lambda A, x=x, a=a, b=b: A(R("VH", a, b))[0:128:16, :], [R("VH", a, b)], [R(x, 0, 1)],
+               "d%d" % k, [], 0.0)
+            gd("ss", lambda A, y=y: A(y)[r], lambda A, a=a, b=b: A(R("VH", a, b, 1, 16 * r, 16 * r + 1)), [R("VH", a, b)], [R(y, 0, 1)],
+               "d%d" % (k + 1), [], 0.0)
+            op(L, "g", 1.5, [R(x, 0, 1)], [R(x, 1, 2)], lambda Q, A, x=x, y=y, z=z: Q["values"](x, y, z))
+            gd("sy", lambda A, a=a, b=b: A(R("V8", a, b, 1, 0, 8)), lambda A, y=y: A(y), [R(y, 0, 1), R(x, 1, 2)], [R("V8", a, b, 1, 0, 8)],
+               "d%d" % (k + 2), [(z, N - 1)], 2.5)
     for c in range(4):
         mm(L, R("b%d" % (4 + c), 128, 256), [(R("S8", 0, 128, 1, 0, 8), R("V8", 128 * c, 128 * c + 128, 1, 0, 8))])
         act(L, R("F%d" % c, 128, 256), R("b%d" % (4 + c), 128, 256))
@@ -479,7 +490,7 @@ def program(r, arrive):
             mm(L, bk(1 + m, 1), [(one, row(512 + 128 * cl[m])), (ckf("CKa", m, m), kL)])
             offsets(L, m, sx, bk(1 + m, 0), bk(1 + m, 1))
             look(L, m)
-        mm(L, bk(3, 3), [(R("DM", 0, 128), Fh)])
+        mm(L, bk(2, 3), [(R("DM", 0, 128), Fh)])
         for m in range(3):
             mm(L, bk(0, m), [(R("RI", 0, 128, 1, 0, 2), R("OB", 0, 128, 1, 0, 2)), (kL, ckf("CK", m, m))])
         op(L, "s", 0.12, [R("b0", 0, 384, 16), R("IC", 0, 1)], [R("KTs", 0, 24)], lambda Q, A: [Q["s"].activation(
@@ -524,8 +535,8 @@ def program(r, arrive):
             tt(L, at("WB", m), kb, bk(7, m), al.is_equal)
             mm(L, bk(1 + m, 0), [(at("WB", m), ckf("CK", 0, m))])
             ts(L, at("WK", m), bk(1 + m, 0), R("IW", 0, 1), None, al.mult)
-            mms(L, bk(4 + m, 0), [(R("EH", 1024 * m + 128 * q, 1024 * m + 128 * q + 128), R("WK", 128 * m + 16 * q, 128 * m + 16 * q + 16)) for q in range(8)])
-            tt(L, at("MJ", m), bk(4 + m, 0), at("ML", m), al.mult)
+            mms(L, bk(1 + m, 1), [(R("EH", 1024 * m + 128 * q, 1024 * m + 128 * q + 128), R("WK", 128 * m + 16 * q, 128 * m + 16 * q + 16)) for q in range(8)])
+            tt(L, at("MJ", m), bk(1 + m, 1), at("ML", m), al.mult)
             b16 = R("b0", 384 + 16 * m, 400 + 16 * m)
             mm(L, b16, [(at("MJ", m), R("CS", 0, 16)), (R("IDh", 0, 128), R("AD", 0, 16))])
             tt(L, at("LX", m, 16), b16, R("DK", 0, 16), al.max)
@@ -534,17 +545,17 @@ def program(r, arrive):
             gather(L, R(new, 0, 256), R(tile[cl[m]], 0, 512), at("LW", m, 16), "s")
             tile[cl[m]] = new
         ts(L, R("H1", 0, 128), kb, R("S1", 0, 1), R("S2", 0, 1), al.mult, al.is_gt)
-        tt(L, R("HD", 0, 128), R("H1", 0, 128), bk(3, 3), al.mult)
-        mm(L, bk(2, 3), [(R("BOf", 112, 240), R("HD", 0, 128))])
-        cp(L, R("P%d" % (t + 1), 0, 128), bk(2, 3))
-        mm(L, bk(1, 2), [(one, R("OB", 0, 128, 1, 0, 1))] + [(R("NI", 0, 128), at("WB", m)) for m in range(3)])
-        tt(L, at("TM", 3), bk(1, 2), at("SX", 0), al.mult)
+        tt(L, R("HD", 0, 128), R("H1", 0, 128), bk(2, 3), al.mult)
+        mm(L, bk(7, 0), [(R("BOf", 112, 240), R("HD", 0, 128))])
+        cp(L, R("P%d" % (t + 1), 0, 128), bk(7, 0))
+        mm(L, bk(5, 1), [(one, R("OB", 0, 128, 1, 0, 1))] + [(R("NI", 0, 128), at("WB", m)) for m in range(3)])
+        tt(L, at("TM", 3), bk(5, 1), at("SX", 0), al.mult)
         for m in range(3):
-            mm(L, bk(1 + m, 1), [(fwd("IDb", m), at("WB", m))])
-            tt(L, at("TM", m), bk(1 + m, 1), R("R", 384 * m, 384 * m + 128), al.mult)
+            mm(L, bk(4 + m, 0), [(fwd("IDb", m), at("WB", m))])
+            tt(L, at("TM", m), bk(4 + m, 0), R("R", 384 * m, 384 * m + 128), al.mult)
         mm(L, bk(3, 2), [(R("IDf", 0, 128), at("TM", 3))] + [(bwd("IDf", m), at("TM", m)) for m in range(3)])
         act(L, FB, bk(3, 2))
-        own_value(L, t, 3, bk(3, 2), bk(1, 3), FV, "tab")
+        own_value(L, t, 3, bk(3, 2), bk(7, 3), FV, "tab")
     marks.append(len(L))
     for c in range(4):
         mm(L, R("b%d" % (4 + c), 0, 128), [(R("REV", 0, 128), R(tile[c], 0, 128))])
@@ -639,7 +650,10 @@ def rank_program(g, core, T, topo):
     for n, (kind, s, k) in enumerate(seq):
         q = (g.sync, g.scalar)[n % 2]
         q.dma_start(T["xs"][s], T["sight"][16 * s:16 * s + 16, :]).then_inc(T.sem["m%d" % n], 16)
+        if n == 0:
+            g.sync.dma_start(T["BH"][:], T["bun"][:]).then_inc(T.sem["d21"], 16)
         if n == 1:
+            g.scalar.dma_start(T["tabH"][:, 0:4096], T["sight"][:]).then_inc(T.sem["d22"], 16)
             g.sync.dma_start(T["bs"][:], T["bun"][:]).then_inc(T.sem["m7"], 16)
             g.scalar.dma_start(T["qs"][:], T["pots"][:]).then_inc(T.sem["m8"], 16)
             g.sync.dma_start(T["br"][r], T["bun"][16 * r:16 * r + 16, :]).then_inc(T.sem["m9"], 16)
@@ -657,33 +671,35 @@ def rank_program(g, core, T, topo):
                 loc[0] += len(es)
             g.remote_dma_fused(tr, local_sem=T.sem["ls"])
 
-    for n, (kind, s, k) in enumerate(seq):
-        g.wait_ge(T.sem["m%d" % n], 16)
-        if kind == "h":
-            loc[0] += write(p["helper"], T["xr"][k], T["xs"][s], "hx%d" % k, on)
-        else:
-            loc[0] += write(cores[s], T["xr"][r], T["xs"][s], "ax%d" % r, off if kind == "d" else on)
-        if n == 1:
-            g.wait_ge(T.sem["m7"], 16)
-            fused(many, "bs", "br", "ab")
-            g.wait_ge(T.sem["m8"], 16)
-            ids, ds = [], []
-            for d in others:
-                rid, pid = addr(cores[d])
-                ids.append(DstId(rid=rid, pnc=pid))
-                ds.append(T["qr"][r])
-            g.remote_dma_fused([RemoteDMATransfer(dst_ids=ids, dma_engine_mask=bits(off[:1]), remote_sem=T.sem["aq"], srcs=[T["qs"][:]], dsts=ds)],
-                               local_sem=T.sem["ls"])
-            loc[0] += 1
+    def exchange():
+        for n, (kind, s, k) in enumerate(seq):
+            g.wait_ge(T.sem["m%d" % n], 16)
+            if kind == "h":
+                loc[0] += write(p["helper"], T["xr"][k], T["xs"][s], "hx%d" % k, on)
+            else:
+                loc[0] += write(cores[s], T["xr"][r], T["xs"][s], "ax%d" % r, off if kind == "d" else on)
+            if n == 1:
+                g.wait_ge(T.sem["m7"], 16)
+                fused(many, "bs", "br", "ab")
+                g.wait_ge(T.sem["m8"], 16)
+                ids, ds = [], []
+                for d in others:
+                    rid, pid = addr(cores[d])
+                    ids.append(DstId(rid=rid, pnc=pid))
+                    ds.append(T["qr"][r])
+                g.remote_dma_fused([RemoteDMATransfer(dst_ids=ids, dma_engine_mask=bits(off[:1]), remote_sem=T.sem["aq"], srcs=[T["qs"][:]], dsts=ds)],
+                                   local_sem=T.sem["ls"])
+                loc[0] += 1
+        return []
 
     L, marks = program(r, arrive)
     depend(L)
     order, busy = schedule(L, marks)
-    def values():
-        fused(single, "vhs", "vhr", "ah")
+    def values(a, b, s):
+        fused(single, a, b, s)
         return []
 
-    Q = {"values": values, "v": g.vector, "s": g.scalar, "pe": g.tensor, "g": g, "sy": g.sync, "ss": g.scalar, "who": [None]}
+    Q = {"exchange": exchange, "values": values, "v": g.vector, "s": g.scalar, "pe": g.tensor, "g": g, "sy": g.sync, "ss": g.scalar, "who": [None]}
 
     def A(x):
         if isinstance(x, str):

@@ -10,25 +10,25 @@ F32, BF, I32, U16, F16 = "float32", "bfloat16", "int32", "uint16", "float16"
 
 SCRATCH = {
     "xs": ("dram", [8, 128, 512], BF), "xr": ("dram", [8, 128, 512], BF),
-    "bs": ("dram", [8, 128, 64], I32), "br": ("dram", [8, 128, 64], I32),
+    "bs": ("dram", [8, 128, 64], U16), "br": ("dram", [8, 128, 64], U16),
     "qs": ("dram", [128, 8], I32), "qr": ("dram", [8, 128, 8], I32),
     "ys": ("dram", [8, 128, 64], F32), "yr": ("dram", [8, 128, 64], F32),
     "vs": ("dram", [8, 128, 4], F32), "vr": ("dram", [8, 128, 4], F32),
     "ws": ("dram", [8, 128, 1], F32), "wr": ("dram", [8, 128, 1], F32),
     "tab": ("sbuf", [128, 4112], BF),
-    "BI": ("sbuf", [128, 512], I32), "BA": ("sbuf", [128, 512], F32), "BB": ("sbuf", [128, 512], F32), "BT": ("sbuf", [128, 512], F32),
+    "BI": ("sbuf", [128, 512], U16), "BU": ("sbuf", [128, 512], U16), "BA": ("sbuf", [128, 512], F32), "BB": ("sbuf", [128, 512], F32), "BT": ("sbuf", [128, 512], F32),
     "PI": ("sbuf", [8, 128], I32), "PB": ("sbuf", [8, 128], F32), "PC": ("sbuf", [8, 128], F32),
     "Y": ("sbuf", [128, 512], F32), "VY": ("sbuf", [128, 512], F32), "PO": ("sbuf", [128, 128], F32),
     "OB": ("sbuf", [128, 512], BF), "OFm": ("sbuf", [128, 256], F32),
     "IDf": ("sbuf", [128, 256], F32), "IDb": ("sbuf", [128, 256], BF), "IDa": ("sbuf", [128, 256], F16), "IDp": ("sbuf", [128, 256], F16),
-    "IDh": ("sbuf", [128, 128], F16), "BOh": ("sbuf", [128, 128], F16), "Fh": ("sbuf", [128, 128], F16), "ID2": ("sbuf", [128, 256], F32),
+    "IDh": ("sbuf", [128, 256], F16), "BOh": ("sbuf", [128, 128], F16), "Fh": ("sbuf", [128, 128], F16), "ID2": ("sbuf", [128, 256], F32),
     "REV": ("sbuf", [128, 128], F32), "BOb": ("sbuf", [128, 256], BF), "BO4": ("sbuf", [128, 256], BF), "BOf": ("sbuf", [128, 256], F32),
     "CK": ("sbuf", [128, 768], BF), "CKm": ("sbuf", [128, 768], BF), "CKa": ("sbuf", [128, 768], BF),
     "SD": ("sbuf", [128, 2048], BF), "NEG": ("sbuf", [128, 256], BF), "Wq": ("sbuf", [128, 1024], BF),
-    "PW": ("sbuf", [128, 128], F32), "HF": ("sbuf", [128, 128], F32), "ZF": ("sbuf", [128, 128], F32),
+    "PW": ("sbuf", [128, 128], F32),
     "SM": ("sbuf", [128, 88], F32), "SI": ("sbuf", [128, 16], I32), "MJ": ("sbuf", [128, 384], F16), "DK": ("sbuf", [128, 16], F32),
     "AD": ("sbuf", [128, 16], F16), "LX": ("sbuf", [128, 48], F32), "IOK": ("sbuf", [128, 128], BF), "I16": ("sbuf", [128, 384], BF), "ML": ("sbuf", [128, 384], F32),
-    "CS": ("sbuf", [128, 24], F16), "DL": ("sbuf", [128, 24], F16), "RI": ("sbuf", [128, 128], BF),
+    "CS": ("sbuf", [128, 24], F16), "DL": ("sbuf", [128, 24], F16), "RI": ("sbuf", [128, 256], BF),
     "CR": ("sbuf", [128, 1408], BF), "DM": ("sbuf", [128, 128], F16), "DS": ("sbuf", [128, 128], F32),
     "MUS": ("sbuf", [128, 512], F32), "A3S": ("sbuf", [128, 512], F32), "RM": ("sbuf", [128, 2048], BF), "S8": ("sbuf", [128, 128], F32),
     "G": ("sbuf", [128, 8192], BF), "Z": ("sbuf", [128, 8192], BF), "SVs": ("sbuf", [128, 384], F32),
@@ -39,13 +39,14 @@ SCRATCH = {
     "kS": ("sbuf", [128, 128], I32), "kT": ("sbuf", [128, 128], I32), "kU": ("sbuf", [128, 128], I32), "kL": ("sbuf", [128, 128], BF),
     "KM": ("sbuf", [128, 384], F16), "KTs": ("sbuf", [128, 24], BF), "LK": ("sbuf", [128, 96], U16), "EH": ("sbuf", [128, 3072], BF),
     "R": ("sbuf", [128, 1152], F32), "NF": ("sbuf", [128, 384], BF), "IN": ("sbuf", [128, 384], BF), "HS": ("sbuf", [128, 384], F16), "KB": ("sbuf", [128, 384], F32),
-    "WB": ("sbuf", [128, 384], BF), "WK": ("sbuf", [128, 384], BF), "LW": ("sbuf", [128, 48], U16), "TM": ("sbuf", [128, 512], F32),
+    "WB": ("sbuf", [128, 384], BF), "WK": ("sbuf", [128, 384], BF), "LW": ("sbuf", [128, 48], U16), "RH": ("sbuf", [128, 512], F32), "TH": ("sbuf", [128, 512], F16),
     "H1": ("sbuf", [128, 128], F32), "HD": ("sbuf", [128, 128], F32),
 }
 for _k in range(4):
     SCRATCH["F%d" % _k] = ("sbuf", [128, 640], F32)
     SCRATCH["E%d" % _k] = ("sbuf", [128, 640], F32)
-SMALL = dict([(_n, ("SM", 8 * _k)) for _k, _n in enumerate(["WC", "DLi", "XF", "IC", "Z0", "Z1", "S1", "S2", "S3", "IW"])] + [("PX", ("SI", 0)), ("XI", ("SI", 8))])
+SMALL = dict([(_n, ("SM", 8 * _k)) for _k, _n in enumerate(["WC", "DLi", "XF", "IC", "Z0", "Z1", "S1", "S2", "S3", "IW"])] + [
+    ("PX", ("SI", 0)), ("XI", ("SI", 8)), ("HF", ("RH", 0)), ("ZF", ("HD", 0)), ("BF", ("VY", 0)), ("RY", ("RI", 128))])
 for _n, _d in (("SX", F32), ("pi", I32), ("pj", I32), ("pk", I32), ("pl", I32), ("of", U16)):
     SCRATCH[_n] = ("sbuf", [128, 512], _d)
 for _k in range(5):
@@ -56,8 +57,8 @@ SEMAPHORES = (["aa", "ah", "ev", "es", "ep", "eg", "ab", "aq", "ay", "aw", "av",
               + ["m%d" % k for k in range(16)] + ["d%d" % k for k in range(30)])
 ESEM = {"v": "ev", "s": "es", "pe": "ep", "g": "eg"}
 CYC = 0.00095
-BONUS = {148:-35,134:-38,27:-55,105:25,25:-30,129:-9,3:-24,146:-24,94:-16,93:-9,131:-35,133:-42,127:-10,154:33,88:-84,35:-43,106:12,155:-7,104:-50,40:-24,2:-25,73:32,29:-28,121:-30,125:-29,144:48,158:28,52:-5,61:-49,128:-7,109:-30,1080:-15,23:22,1077:-2,1143:20,1037:-2,110:20,1026:-5,1027:-8,1173:7,80:-20,1024:5,1012:-20,1150:20,45:18,1107:-5,1160:-2,1152:-5,42:2,1066:-2,1008:-10,1149:2,135:-10,1042:-2,53:2,64:10}
-WHERE = "svsvsvsssssvvssssssvvssv"
+BONUS = {152:-84,138:-38,31:-58,109:67,133:-29,98:-23,135:-55,110:40,44:-48,125:-41,65:-60,132:-21,113:-30,1087:-20,1076:-25,1027:-20,1040:-20,118:33,150:-12,1118:-5,1038:-28,130:-26,51:-30,137:-28,1042:10,1098:-5,107:-45,1198:5,64:-27,134:-6,1059:-10,1079:-15,136:-29,1120:-7,1108:-7,1057:-10,1014:-20,1013:-5,1055:-5,1157:-2,1172:-10,146:12,1170:-10,1031:5,145:42,1092:5,32:3,25:-25,1096:-20,73:-20,29:-5,1075:5,1181:-10,117:39,1045:-30,1052:8,77:-18,47:-5,1069:20,1068:-10,1100:30,1067:-20,1048:20,1166:-2,139:2,85:5,1077:20,97:15,1097:20,122:-18,1029:2,1050:5,1051:20,84:22,2115:-10,161:10,2117:2,1091:25}
+WHERE = "svvvsssssssvvssssssvvssv"
 
 
 def R(name, c0, c1, step=1, p0=0, p1=128):
@@ -132,7 +133,7 @@ def mm(L, out, pairs):
     c = 0.05
     rd = []
     for l, r in pairs:
-        c += max(64, ncols(r)) * 0.0006 * (1 if two(l) else 4)
+        c += max(64, ncols(r)) * 0.00072 * (1 if two(l) else 4)
         rd += [l, r]
 
     def emit(Q, A):
@@ -153,7 +154,7 @@ def gather(L, out, win, off, eng):
 
 def mms(L, out, pairs):
     w = ncols(out) // len(pairs)
-    return op(L, "pe", 0.05 + 64 * len(pairs) * 0.0006, [x for p in pairs for x in p], [out],
+    return op(L, "pe", 0.05 + 64 * len(pairs) * 0.00072, [x for p in pairs for x in p], [out],
               lambda Q, A: [Q["pe"].matmul(A(sub(out, w * k, w * k + w - ncols(out))), A(p[0]), A(p[1]), True, True) for k, p in enumerate(pairs)], n=len(pairs))
 
 
@@ -215,7 +216,7 @@ def schedule(L, marks, hop=0.12, bonus=None, where=None):
         prio[i] = L[i]["cost"] + max([prio[k] + hop for k in succ[i]] + [0.0])
     for a, b in zip(marks, marks[1:]):
         for i in range(a, b):
-            prio[i] += bonus.get(b - i, 0)
+            prio[i] += bonus.get(b - i, 0) + (bonus.get(2000 + b - i, 0) if b == marks[-1] else 0)
     for i in range(marks[0]):
         prio[i] += L[i].get("boost", bonus.get(1000 + i, 0))
     free = {"v": 0.0, "s": 0.0, "pe": 0.0, "g": 0.0, "sy": 0.0, "ss": 0.0}
@@ -327,7 +328,7 @@ def constants(L):
     fill(L, R("ID2", 0, 256, 16), 0.0)
     cp(L, R("IDa", 0, 256), R("ID2", 0, 256))
     tt(L, R("IDp", 0, 256), R("IDf", 0, 256), R("ID2", 0, 256), al.subtract)
-    cp(L, R("IDh", 0, 128), R("IDf", 0, 128))
+    cp(L, R("IDh", 0, 256), R("IDf", 0, 256))
     cp(L, R("BOh", 0, 128), R("BOb", 0, 128))
     act(L, R("CKm", 0, 768), R("CK", 0, 768), 0.0, 32.0)
     act(L, R("CKa", 0, 768), R("CK", 0, 768), 0.0, 148.0)
@@ -366,6 +367,8 @@ def constants(L):
     tt(L, R("HB", 0, 128), R("IDf", 0, 128), R("DT", 0, 128), al.subtract)
     act(L, R("MB", 0, 128), R("DT", 0, 128), 0.0, -8192.0)
     act(L, R("NI", 0, 128), R("IDf", 0, 128), 0.0, -1.0)
+    fill(L, R("RY", 0, 128, 1, 0, 2), -1.0)
+    fill(L, R("RY", 0, 128, 1, 0, 1), 2048.0)
     fill(L, R("RZ", 0, 128, 1, 0, 2), -1.0)
     fill(L, R("RZ", 0, 128, 1, 0, 1), 7936.0)
     ts(L, R("Z0", 0, 1), R("XF", 0, 1), 0.0, None, al.is_equal)
@@ -420,7 +423,6 @@ def program(r, arrive):
     constants(L)
     gd = lambda q, out, in_, reads, writes, sem, ext, rel: op(
         L, q, 2.2, reads, writes, lambda Q, A: [Q[q].dma_start(out(A), in_(A))], sem=sem, ext=ext, rel=rel)
-    gd("sy", lambda A: A(R("BI", 0, 512)), lambda A: A("br"), [], [R("BI", 0, 512)], "d0", [("ab", arrive["ab"]), ("m9", 16)], 9.0)
     gd("sy", lambda A: A(R("PI", 0, 128, 1, 0, 8)), lambda A: A("qr")[:, 16 * r:16 * r + 16, :], [], [R("PI", 0, 128, 1, 0, 8)], "d1",
        [("aq", arrive["aq"]), ("m10", 16)], 9.0)
     gd("ss", lambda A: A(R("tab", 0, 4096, 1, 16 * r, 16 * r + 16)), lambda A: A("sight")[16 * r:16 * r + 16, :], [],
@@ -430,6 +432,11 @@ def program(r, arrive):
            [R("tab", 0, 4096, 1, 16 * s, 16 * s + 16)], "d%d" % (3 + n), [("ax%d" % s, cnt)], 10.0 + n)
     op(L, "sy", 3.5, [], [R("BH", 0, 512)], lambda Q, A: [], sem="d21")
     op(L, "ss", 6.0, [], [R("tabH", 0, 4096)], lambda Q, A: [], sem="d22")
+    ts(L, R("BU", 0, 512), R("BH", 0, 512), 1.0, None, al.add)
+    gd("sy", lambda A: A("bs"), lambda A: A(R("BU", 0, 512)), [R("BU", 0, 512)], [R("bs", 0, 1)], "d0", [], 0.0)
+    gd("sy", lambda A: A("br")[r], lambda A: A(R("BU", 0, 512, 1, 16 * r, 16 * r + 16)), [R("BU", 0, 512)], [R("br", 0, 1)], "d29", [], 0.0)
+    L[op(L, "g", 1.5, [R("bs", 0, 1)], [R("bs", 1, 2)], lambda Q, A: Q["values"]("bs", "br", "ab"))]["boost"] = 1000
+    gd("sy", lambda A: A(R("BI", 0, 512)), lambda A: A("br"), [R("br", 0, 1), R("bs", 1, 2)], [R("BI", 0, 512)], "m7", [("ab", arrive["ab"])], 2.5)
     ts(L, R("BB", 0, 512), R("BH", 0, 512), 0.0, 1.0 - OFF, al.is_lt, al.mult)
     tt(L, R("HC", 0, 512), R("BH", 0, 512), R("BB", 0, 512), al.add)
     for c in range(4):
@@ -448,11 +455,12 @@ def program(r, arrive):
     for c in range(4):
         mm(L, R("b%d" % (4 + c), 128, 256), [(R("S8", 0, 128, 1, 0, 8), R("V8", 128 * c, 128 * c + 128, 1, 0, 8))])
         act(L, R("F%d" % c, 128, 256), R("b%d" % (4 + c), 128, 256))
-    ts(L, R("BA", 0, 512), R("BI", 0, 512), 0.0, 1.0 - OFF, al.is_lt, al.mult)
-    tt(L, R("BT", 0, 512), R("BI", 0, 512), R("BA", 0, 512), al.add)
+    cp(L, R("BF", 0, 512), R("BI", 0, 512))
+    ts(L, R("BA", 0, 512), R("BF", 0, 512), 0.0, 1.0 - OFF, al.is_equal, al.mult)
+    tt(L, R("BT", 0, 512), R("BF", 0, 512), R("BA", 0, 512), al.add)
     for c in range(4):
         mm(L, R("b%d" % (4 + c), 0, 128), [(R("REV", 0, 128), R("BT", c, 512, 4))])
-        act(L, R("F%d" % c, 0, 128), R("b%d" % (4 + c), 0, 128))
+        act(L, R("F%d" % c, 0, 128), R("b%d" % (4 + c), 0, 128), -1.0)
     p8 = lambda nm: R(nm, 0, 128, 1, 0, 8)
     ts(L, p8("PB"), p8("PI"), 0.0, 1.0 - OFF, al.is_lt, al.mult)
     tt(L, p8("PC"), p8("PI"), p8("PB"), al.add)
@@ -548,12 +556,15 @@ def program(r, arrive):
         tt(L, R("HD", 0, 128), R("H1", 0, 128), bk(2, 3), al.mult)
         mm(L, bk(7, 0), [(R("BOf", 112, 240), R("HD", 0, 128))])
         cp(L, R("P%d" % (t + 1), 0, 128), bk(7, 0))
+        for m in range(4):
+            act(L, at("RH", m), at("R", m, 384)[:2] + (384 * m + 128, 1, 0, 128) if m < 3 else at("SX", 0), -SH)
         mm(L, bk(5, 1), [(one, R("OB", 0, 128, 1, 0, 1))] + [(R("NI", 0, 128), at("WB", m)) for m in range(3)])
-        tt(L, at("TM", 3), bk(5, 1), at("SX", 0), al.mult)
+        tt(L, at("TH", 3), bk(5, 1), at("RH", 3), al.mult)
         for m in range(3):
             mm(L, bk(4 + m, 0), [(fwd("IDb", m), at("WB", m))])
-            tt(L, at("TM", m), bk(4 + m, 0), R("R", 384 * m, 384 * m + 128), al.mult)
-        mm(L, bk(3, 2), [(R("IDf", 0, 128), at("TM", 3))] + [(bwd("IDf", m), at("TM", m)) for m in range(3)])
+            tt(L, at("TH", m), bk(4 + m, 0), at("RH", m), al.mult)
+        mm(L, bk(3, 2), [(R("RY", 0, 128, 1, 0, 2), R("OB", 0, 128, 1, 0, 2)), (R("IDh", 0, 128), at("TH", 3))]
+           + [(bwd("IDh", m), at("TH", m)) for m in range(3)])
         act(L, FB, bk(3, 2))
         own_value(L, t, 3, bk(3, 2), bk(7, 3), FV, "tab")
     marks.append(len(L))
@@ -622,7 +633,8 @@ def rank_program(g, core, T, topo):
             n = 0
             for k, s in enumerate(p["helped"]):
                 es = topo.engines(core, cores[s])
-                g.wait_ge(T.sem["hx%d" % k], 8)
+                on = [x for x in topo.engines(cores[r], core) if x not in topo.engines(cores[r], cores[s])]
+                g.wait_ge(T.sem["hx%d" % k], len(on))
                 n += write(cores[s], T["xr"][r], T["xr"][k], "ax%d" % r, es)
             g.wait_ge(T.sem["ls"], n)
         return
@@ -639,14 +651,15 @@ def rank_program(g, core, T, topo):
                     return len(es)
 
     others = [s for s in range(N) if s != r]
-    arrive = {"ab": sum(cnt(s, r, 0) for s in others), "aq": len(others)}
+    arrive = {"ab": len(others), "aq": len(others)}
     first = [s for s in others if s == p["mate"] or r in pl[s]["direct"]]
-    arrive["x"] = [(s, len(on) if s == p["mate"] else 8) for s in first + [s for s in others if s not in first]]
+    late = len(topo.engines(p["helper"], cores[p["away"][0]]))
+    arrive["x"] = [(s, len(on) if s == p["mate"] else late) for s in first + [s for s in others if s not in first]]
 
     seq = []
     for k in range(3):
         seq += [("h", p["helped"][k], k), ("d", p["direct"][k], k)]
-    seq.append(("m", p["mate"], 0))
+    seq.append(("m", p["mate"], 3))
     for n, (kind, s, k) in enumerate(seq):
         q = (g.sync, g.scalar)[n % 2]
         q.dma_start(T["xs"][s], T["sight"][16 * s:16 * s + 16, :]).then_inc(T.sem["m%d" % n], 16)
@@ -654,9 +667,8 @@ def rank_program(g, core, T, topo):
             g.sync.dma_start(T["BH"][:], T["bun"][:]).then_inc(T.sem["d21"], 16)
         if n == 1:
             g.scalar.dma_start(T["tabH"][:, 0:4096], T["sight"][:]).then_inc(T.sem["d22"], 16)
-            g.sync.dma_start(T["bs"][:], T["bun"][:]).then_inc(T.sem["m7"], 16)
+        if n == 6:
             g.scalar.dma_start(T["qs"][:], T["pots"][:]).then_inc(T.sem["m8"], 16)
-            g.sync.dma_start(T["br"][r], T["bun"][16 * r:16 * r + 16, :]).then_inc(T.sem["m9"], 16)
             g.scalar.dma_start(T["qr"][r], T["pots"][:]).then_inc(T.sem["m10"], 16)
     tot = {}
     loc = [0]
@@ -672,24 +684,27 @@ def rank_program(g, core, T, topo):
             g.remote_dma_fused(tr, local_sem=T.sem["ls"])
 
     def exchange():
-        for n, (kind, s, k) in enumerate(seq):
-            g.wait_ge(T.sem["m%d" % n], 16)
-            if kind == "h":
-                loc[0] += write(p["helper"], T["xr"][k], T["xs"][s], "hx%d" % k, on)
-            else:
-                loc[0] += write(cores[s], T["xr"][r], T["xs"][s], "ax%d" % r, off if kind == "d" else on)
-            if n == 1:
-                g.wait_ge(T.sem["m7"], 16)
-                fused(many, "bs", "br", "ab")
-                g.wait_ge(T.sem["m8"], 16)
-                ids, ds = [], []
-                for d in others:
-                    rid, pid = addr(cores[d])
-                    ids.append(DstId(rid=rid, pnc=pid))
-                    ds.append(T["qr"][r])
-                g.remote_dma_fused([RemoteDMATransfer(dst_ids=ids, dma_engine_mask=bits(off[:1]), remote_sem=T.sem["aq"], srcs=[T["qs"][:]], dsts=ds)],
-                                   local_sem=T.sem["ls"])
-                loc[0] += 1
+        for part in range(4):
+            tr = []
+            for n, (kind, s, k) in enumerate(seq):
+                if k == part:
+                    g.wait_ge(T.sem["m%d" % n], 16)
+                    c, slot, sem = (p["helper"], k, "hx%d" % k) if kind == "h" else (cores[s], r, "ax%d" % r)
+                    es = off if kind == "d" else on
+                    rid, pid = addr(c)
+                    tr.append(RemoteDMATransfer(dst_ids=[DstId(rid=rid, pnc=pid)], dma_engine_mask=bits(es), remote_sem=T.sem[sem],
+                                                src=T["xs"][s], dst=T["xr"][slot]))
+                    loc[0] += len(es)
+            g.remote_dma_fused(tr, local_sem=T.sem["ls"])
+        g.wait_ge(T.sem["m8"], 16)
+        ids, ds = [], []
+        for d in others:
+            rid, pid = addr(cores[d])
+            ids.append(DstId(rid=rid, pnc=pid))
+            ds.append(T["qr"][r])
+        g.remote_dma_fused([RemoteDMATransfer(dst_ids=ids, dma_engine_mask=bits(off[:1]), remote_sem=T.sem["aq"], srcs=[T["qs"][:]], dsts=ds)],
+                           local_sem=T.sem["ls"])
+        loc[0] += 1
         return []
 
     L, marks = program(r, arrive)
@@ -708,14 +723,14 @@ def rank_program(g, core, T, topo):
         return T[nm][p0:p1, c0:c1] if st == 1 else T[nm][p0:p1, c0:c1:st]
     emit_all(L, order, Q, A, T, tot)
 
-    g.wait_ge(T.sem["d12"], 16)
-    fused(many, "ys", "yr", "ay")
     g.wait_ge(T.sem["d13"], 16)
     fused(single, "ws", "wr", "aw")
+    g.wait_ge(T.sem["d12"], 16)
+    fused(many, "ys", "yr", "ay")
     g.wait_ge(T.sem["d16"], 16)
     fused(single, "vs", "vr", "av")
     g.sync.wait_ge(T.sem["d14"], 16)
-    g.sync.wait_ge(T.sem["ay"], arrive["ab"])
+    g.sync.wait_ge(T.sem["ay"], sum(cnt(s, r, 0) for s in others))
     g.sync.dma_start(T["yb"][:], T["yr"][:]).then_inc(T.sem["d18"], 16)
     g.sync.wait_ge(T.sem["d15"], 16)
     g.sync.wait_ge(T.sem["aw"], len(others))

import numpy as np
from concourse.bass import DstId, RemoteDMATransfer
from concourse.mybir import AluOpType, ActivationFunctionType

N = 8
OFF = 257
MASK = 4095 + (1 << 20)
SH = 2047.0
F32, BF, I32, U16, F16 = "float32", "bfloat16", "int32", "uint16", "float16"

SCRATCH = {
    "xs": ("dram", [8, 128, 512], BF), "xr": ("dram", [8, 128, 512], BF),
    "bs": ("dram", [8, 128, 64], U16), "br": ("dram", [8, 128, 64], U16),
    "qs": ("dram", [128, 8], I32), "qr": ("dram", [8, 128, 8], I32),
    "ys": ("dram", [8, 128, 64], F32), "yr": ("dram", [8, 128, 64], F32),
    "vs": ("dram", [8, 128, 4], F32), "vr": ("dram", [8, 128, 4], F32),
    "ws": ("dram", [8, 128, 1], F32), "wr": ("dram", [8, 128, 1], F32),
    "tab": ("sbuf", [128, 4112], BF),
    "BI": ("sbuf", [128, 512], U16), "BU": ("sbuf", [128, 512], U16), "BA": ("sbuf", [128, 512], F32), "BB": ("sbuf", [128, 512], F32), "BT": ("sbuf", [128, 512], F32),
    "PI": ("sbuf", [8, 128], I32), "PB": ("sbuf", [8, 128], F32), "PC": ("sbuf", [8, 128], F32),
    "Y": ("sbuf", [128, 512], F32), "VY": ("sbuf", [128, 512], F32), "PO": ("sbuf", [128, 128], F32),
    "OB": ("sbuf", [128, 512], BF), "OFm": ("sbuf", [128, 256], F32),
    "IDf": ("sbuf", [128, 256], F32), "IDb": ("sbuf", [128, 256], BF), "IDa": ("sbuf", [128, 256], F16), "IDp": ("sbuf", [128, 256], F16),
    "IDh": ("sbuf", [128, 256], F16), "BOh": ("sbuf", [128, 128], F16), "Fh": ("sbuf", [128, 128], F16), "ID2": ("sbuf", [128, 256], F32),
    "REV": ("sbuf", [128, 128], F32), "BOb": ("sbuf", [128, 256], BF), "BO4": ("sbuf", [128, 256], BF), "BOf": ("sbuf", [128, 256], F32),
    "CK": ("sbuf", [128, 768], BF), "CKm": ("sbuf", [128, 768], BF), "CKa": ("sbuf", [128, 768], BF),
    "SD": ("sbuf", [128, 2048], BF), "NEG": ("sbuf", [128, 256], BF), "Wq": ("sbuf", [128, 1024], BF),
    "PW": ("sbuf", [128, 128], F32),
    "SM": ("sbuf", [128, 88], F32), "SI": ("sbuf", [128, 16], I32), "MJ": ("sbuf", [128, 384], F16), "DK": ("sbuf", [128, 16], F32),
    "AD": ("sbuf", [128, 16], F16), "LX": ("sbuf", [128, 48], F32), "IOK": ("sbuf", [128, 128], BF), "I16": ("sbuf", [128, 384], BF), "ML": ("sbuf", [128, 384], F32),
    "CS": ("sbuf", [128, 24], F16), "DL": ("sbuf", [128, 24], F16), "RI": ("sbuf", [128, 256], BF),
    "CR": ("sbuf", [128, 1408], BF), "DM": ("sbuf", [128, 128], F16), "DS": ("sbuf", [128, 128], F32),
    "MUS": ("sbuf", [128, 512], F32), "A3S": ("sbuf", [128, 512], F32), "RM": ("sbuf", [128, 2048], BF), "S8": ("sbuf", [128, 128], F32),
    "G": ("sbuf", [128, 8192], BF), "Z": ("sbuf", [128, 8192], BF), "SVs": ("sbuf", [128, 384], F32),
    "HB": ("sbuf", [128, 128], BF), "MB": ("sbuf", [128, 128], BF), "DT": ("sbuf", [128, 128], F32), "RZ": ("sbuf", [128, 128], BF),
    "NI": ("sbuf", [128, 128], BF), "tabH": ("sbuf", [128, 4112], BF), "BH": ("sbuf", [128, 512], I32), "HC": ("sbuf", [128, 512], F32),
    "VH": ("sbuf", [128, 512], F32), "V8": ("sbuf", [8, 512], F32), "vhs": ("dram", [8, 128, 3], F32), "vhr": ("dram", [8, 128, 3], F32),
    "vas": ("dram", [8, 128, 1], F32), "var": ("dram", [8, 128, 1], F32),
    "kS": ("sbuf", [128, 128], I32), "kT": ("sbuf", [128, 128], I32), "kU": ("sbuf", [128, 128], I32), "kL": ("sbuf", [128, 128], BF),
    "KM": ("sbuf", [128, 384], F16), "KTs": ("sbuf", [128, 24], BF), "LK": ("sbuf", [128, 96], U16), "EH": ("sbuf", [128, 3072], BF),
    "R": ("sbuf", [128, 1152], F32), "NF": ("sbuf", [128, 384], BF), "IN": ("sbuf", [128, 384], BF), "HS": ("sbuf", [128, 384], F16), "KB": ("sbuf", [128, 384], F32),
    "WB": ("sbuf", [128, 384], BF), "WK": ("sbuf", [128, 384], BF), "LW": ("sbuf", [128, 48], U16), "RH": ("sbuf", [128, 512], F32), "TH": ("sbuf", [128, 512], F16),
    "H1": ("sbuf", [128, 128], F32), "HD": ("sbuf", [128, 128], F32),
}
for _k in range(4):
    SCRATCH["F%d" % _k] = ("sbuf", [128, 640], F32)
    SCRATCH["E%d" % _k] = ("sbuf", [128, 640], F32)
SMALL = dict([(_n, ("SM", 8 * _k)) for _k, _n in enumerate(["WC", "DLi", "XF", "IC", "Z0", "Z1", "S1", "S2", "S3", "IW"])] + [
    ("PX", ("SI", 0)), ("XI", ("SI", 8)), ("HF", ("RH", 0)), ("ZF", ("HD", 0)), ("BF", ("VY", 0)), ("RY", ("RI", 128))])
for _n, _d in (("SX", F32), ("pi", I32), ("pj", I32), ("pk", I32), ("pl", I32), ("of", U16)):
    SCRATCH[_n] = ("sbuf", [128, 512], _d)
for _k in range(5):
    SCRATCH["P%d" % _k] = ("sbuf", [128, 128], F16)
for _k in range(8):
    SCRATCH["b%d" % _k] = ("psum", [128, 512], F32)
SEMAPHORES = (["aa", "ah", "ev", "es", "ep", "eg", "ab", "aq", "ay", "aw", "av", "ls"] + ["ax%d" % k for k in range(8)] + ["hx%d" % k for k in range(3)]
              + ["m%d" % k for k in range(16)] + ["d%d" % k for k in range(30)])
ESEM = {"v": "ev", "s": "es", "pe": "ep", "g": "eg"}
CYC = 0.00095
BONUS = {152:-84,138:-38,31:-58,109:67,133:-29,98:-23,135:-55,110:40,44:-48,125:-41,65:-60,132:-21,113:-30,1087:-20,1076:-25,1027:-20,1040:-20,118:33,150:-12,1118:-5,1038:-28,130:-26,51:-30,137:-28,1042:10,1098:-5,107:-45,1198:5,64:-27,134:-6,1059:-10,1079:-15,136:-29,1120:-7,1108:-7,1057:-10,1014:-20,1013:-5,1055:-5,1157:-2,1172:-10,146:12,1170:-10,1031:5,145:42,1092:5,32:3,25:-25,1096:-20,73:-20,29:-5,1075:5,1181:-10,117:39,1045:-30,1052:8,77:-18,47:-5,1069:20,1068:-10,1100:30,1067:-20,1048:20,1166:-2,139:2,85:5,1077:20,97:15,1097:20,122:-18,1029:2,1050:5,1051:20,84:22,2115:-10,161:10,2117:2,1091:25}
WHERE = "svvvsssssssvvssssssvvssv"


def R(name, c0, c1, step=1, p0=0, p1=128):
    if name in SMALL:
        name, o = SMALL[name]
        c0, c1 = c0 + o, c1 + o
    return (name, c0, c1, step, p0, p1)


def sub(r, a, b):
    return (r[0], r[1] + a, r[2] + b, r[3], r[4], r[5])


def ncols(r):
    return (r[2] - r[1] + r[3] - 1) // r[3]


def two(r):
    return SCRATCH[r[0]][2] in (BF, U16, F16)


def psum(r):
    return SCRATCH[r[0]][0] == "psum"


def meet(a, b):
    if a[1] >= b[2] or b[1] >= a[2] or a[4] >= b[5] or b[4] >= a[5]:
        return False
    return not (a[3] == b[3] and a[3] > 1 and (a[1] - b[1]) % a[3])


def op(L, eng, cost, reads, writes, emit, sem=None, ext=None, rel=0.0, n=1):
    L.append({"eng": eng, "cost": cost, "r": reads, "w": writes, "emit": emit, "sem": sem, "ext": ext or [], "rel": rel, "n": n})
    return len(L) - 1


def refs(*xs):
    return [x for x in xs if isinstance(x, tuple)]


def tt(L, out, a, b, o):
    k = 1 if psum(a) or psum(b) else 2
    return op(L, "v", max(64, ncols(out) * k) * CYC, [a, b], [out],
              lambda Q, A: [Q["v"].tensor_tensor(out=A(out), in0=A(a), in1=A(b), op=o)])


def ts(L, out, a, s1, s2, o0, o1=None):
    k = 0.5 if two(out) and two(a) else 1

    def emit(Q, A):
        kw = {} if o1 is None else {"op1": o1}
        return [Q["v"].tensor_scalar(out=A(out), in0=A(a), scalar1=A(s1) if isinstance(s1, tuple) else s1,
                                     scalar2=A(s2) if isinstance(s2, tuple) else s2, op0=o0, **kw)]
    return op(L, "v", max(64, ncols(out) * k) * CYC, [a] + refs(s1, s2), [out], emit)


def cp(L, out, a):
    k = 0.5 if two(out) and two(a) else 1
    return op(L, "v", max(64, ncols(out) * k) * CYC, [a], [out], lambda Q, A: [Q["v"].tensor_copy(out=A(out), in_=A(a))])


def act(L, out, a, bias=0.0, scale=1.0):
    return op(L, "s", max(64, ncols(out)) * CYC + 0.05, [a], [out],
              lambda Q, A: [Q["s"].activation(out=A(out), in_=A(a), func=ActivationFunctionType.Identity, bias=bias, scale=scale)])


def fill(L, out, c):
    return op(L, "v", max(64, ncols(out) * (0.5 if two(out) else 1)) * CYC, [], [out], lambda Q, A: [Q["v"].memset(A(out), c)])


def mm(L, out, pairs):
    c = 0.05
    rd = []
    for l, r in pairs:
        c += max(64, ncols(r)) * 0.00072 * (1 if two(l) else 4)
        rd += [l, r]

    def emit(Q, A):
        z = None
        for k in range(len(pairs)):
            z = Q["pe"].matmul(A(out), A(pairs[k][0]), A(pairs[k][1]), k == 0, k == len(pairs) - 1)
        return [z]
    return op(L, "pe", c, rd, [out], emit)


def gather(L, out, win, off, eng):
    def emit(Q, A):
        if Q["who"][0] == "v":
            return [Q["v"].tensor_copy(out=A(out), in_=A(win).indirect(A(off)))]
        return [Q["s"].activation(out=A(out), in_=A(win).indirect(A(off)), func=ActivationFunctionType.Identity, bias=0.0, scale=1.0)]
    return op(L, eng, 0.06 + ncols(out) * 1.56 * CYC, [win, off], [out], emit)


def mms(L, out, pairs):
    w = ncols(out) // len(pairs)
    return op(L, "pe", 0.05 + 64 * len(pairs) * 0.00072, [x for p in pairs for x in p], [out],
              lambda Q, A: [Q["pe"].matmul(A(sub(out, w * k, w * k + w - ncols(out))), A(p[0]), A(p[1]), True, True) for k, p in enumerate(pairs)], n=len(pairs))


def asel(L, out, a, pattern, cmp, fillv, base, cm):
    return op(L, "g", 0.2 + ncols(out) * 2 * CYC, [a], [out],
              lambda Q, A: [Q["g"].affine_select(A(out), A(a), pattern, cmp, fillv, base, cm)])


def iota(L, out, pattern, base, cm):
    def emit(Q, A):
        if SCRATCH[out[0]][2] == I32:
            return [Q["g"].iota(A(out), pattern, base, cm)]
        return [Q["g"].iota(A(out), pattern, base, cm, allow_small_or_imprecise_dtypes=True)]
    return op(L, "g", 0.15 + ncols(out) * 2 * CYC, [], [out], emit)


def depend(L):
    hist = {}
    for i, o in enumerate(L):
        pred = {}
        for w, rs in ((False, o["r"]), (True, o["w"])):
            for x in rs:
                keep = []
                for (j, y, yw) in hist.get(x[0], []):
                    if j == i:
                        keep.append((j, y, yw))
                        continue
                    same = L[j]["eng"] == o["eng"]
                    hit = (w or yw) and meet(x, y)
                    if psum(x) and not same:
                        hit = True
                    if hit:
                        pred[j] = True
                    if not (w and y[1] >= x[1] and y[2] <= x[2] and y[4] >= x[4] and y[5] <= x[5] and x[3] == 1 and not psum(x)):
                        keep.append((j, y, yw))
                hist[x[0]] = keep
        for w, rs in ((False, o["r"]), (True, o["w"])):
            for x in rs:
                hist.setdefault(x[0], []).append((i, x, w))
        o["pred"] = pred


def schedule(L, marks, hop=0.12, bonus=None, where=None):
    bonus = BONUS if bonus is None else bonus
    where = WHERE if where is None else where
    n = len(L)
    k = 0
    for o in L:
        if o["eng"] == "vs":
            o["eng"] = where[k if k < 8 else 8 + (k - 8) % 8 if k < 32 else k - 16]
            k += 1
    succ = [[] for _ in range(n)]
    prio = [0.0] * n
    left = [len(o["pred"]) for o in L]
    for i, o in enumerate(L):
        for j in o["pred"]:
            succ[j].append(i)
    for i in range(n - 1, -1, -1):
        prio[i] = L[i]["cost"] + max([prio[k] + hop for k in succ[i]] + [0.0])
    for a, b in zip(marks, marks[1:]):
        for i in range(a, b):
            prio[i] += bonus.get(b - i, 0) + (bonus.get(2000 + b - i, 0) if b == marks[-1] else 0)
    for i in range(marks[0]):
        prio[i] += L[i].get("boost", bonus.get(1000 + i, 0))
    free = {"v": 0.0, "s": 0.0, "pe": 0.0, "g": 0.0, "sy": 0.0, "ss": 0.0}
    at = [o["rel"] for o in L]
    ready = [i for i in range(n) if left[i] == 0]
    order = []
    busy = dict((k, 0.0) for k in free)
    while ready:
        best = None
        for i in ready:
            e = L[i]["eng"]
            key = (max(free[e], at[i]), -prio[i])
            if best is None or key < best[0]:
                best = (key, i, e)
        (t0, _p), i, e = best
        ready.remove(i)
        o = L[i]
        o["eng"] = e
        o["t0"] = t0
        fin = t0 + o["cost"]
        free[e] = fin if e in ESEM else t0 + 0.1
        busy[e] += o["cost"]
        o["t1"] = fin
        order.append(i)
        for k in succ[i]:
            at[k] = max(at[k], fin + hop)
            left[k] -= 1
            if left[k] == 0:
                ready.append(k)
    return order, busy


def emit_all(L, order, Q, A, T, tot):
    known = dict((e, {}) for e in ("v", "s", "pe", "g", "sy", "ss"))
    for i in order:
        o = L[i]
        e = o["eng"]
        q = Q[e]
        kn = known[e]
        need = {}
        for j in o["pred"]:
            p = L[j]
            same = p["eng"] == e and e in ESEM
            if same and not o["pred"][j]:
                continue
            if need.get(p["sem"], (0, None))[0] < p["val"]:
                need[p["sem"]] = (p["val"], j)
        for s in sorted(need, key=lambda z: -L[need[z][1]]["t1"]):
            v, j = need[s]
            if kn.get(s, 0) >= v:
                continue
            q.wait_ge(T.sem[s], v)
            for s2, v2 in L[j]["clock"].items():
                if kn.get(s2, 0) < v2:
                    kn[s2] = v2
        for s, v in o["ext"]:
            q.wait_ge(T.sem[s], v)
        Q["who"][0] = e
        zs = o["emit"](Q, A)
        if e in ESEM:
            s = ESEM[e]
            for z in zs:
                z.then_inc(T.sem[s], 1)
            tot[s] = tot.get(s, 0) + len(zs)
        else:
            s = o["sem"]
            for z in zs:
                z.then_inc(T.sem[s], 16)
            tot[s] = 16
        o["sem"] = s
        o["val"] = tot[s]
        ck = dict(kn)
        ck[s] = tot[s]
        o["clock"] = ck
    return known


def constants(L):
    al = AluOpType
    L[iota(L, R("MUS", 0, 512), [[8, 4], [32, 128]], 5, 0)]["boost"] = 3000
    L[iota(L, R("A3S", 0, 512), [[37, 4], [148, 128]], 0, 0)]["boost"] = 3000
    L[op(L, "g", 4.5, [R("MUS", 0, 512), R("A3S", 0, 512)], [], lambda Q, A: Q["exchange"]())]["boost"] = 2000
    fill(L, R("OB", 0, 512), 1.0)
    fill(L, R("OFm", 0, 256), 1.0)
    fb, ff = R("OB", 0, 256), R("OFm", 0, 256)
    fill(L, R("tab", 4096, 4112), 0.0)
    fill(L, R("tabH", 4096, 4112), 0.0)
    for k in range(4):
        fill(L, R("F%d" % k, 256, 512), 0.0)
        fill(L, R("E%d" % k, 256, 512), 0.0)
    asel(L, R("IDf", 0, 256), ff, [[0, 2], [-1, 128]], al.is_equal, 0.0, 0, 1)
    asel(L, R("REV", 0, 128), R("OFm", 0, 128), [[-16, 8], [1, 16]], al.is_equal, 0.0, -15, 1)
    asel(L, R("S8", 0, 128), R("OFm", 0, 128), [[-1, 8], [0, 16]], al.is_equal, 0.0, 0, 1)
    for m in range(3):
        asel(L, R("CK", 256 * m, 256 * m + 256), fb, [[0, 2], [-16, 8], [0, 16]], al.is_equal, 0.0, -(15 - m), 1)
    asel(L, R("BOb", 0, 256), fb, [[0, 2], [-16, 8], [0, 16]], al.is_ge, 0.0, 0, 1)
    asel(L, R("BOb", 0, 256), R("BOb", 0, 256), [[0, 2], [16, 8], [0, 16]], al.is_ge, 0.0, 15, -1)
    iota(L, R("IOK", 0, 128), [[1, 128]], 0, 0)
    iota(L, R("PX", 0, 1), [[1, 1]], 0, 1)
    asel(L, R("I16", 0, 384), R("OB", 0, 384), [[0, 24], [-1, 16]], al.is_equal, 0.0, 0, 1)
    iota(L, R("DLi", 0, 8), [[16, 8]], 0, 0)
    fill(L, R("RI", 0, 128), -256.0)
    iota(L, R("RI", 0, 128, 1, 0, 1), [[-1, 128]], 0, 0)
    asel(L, R("DS", 0, 128), R("OFm", 0, 128), [[-1, 128]], al.is_equal, 0.0, -1, 1)
    act(L, R("IDb", 0, 256), R("IDf", 0, 256))
    act(L, R("BOf", 0, 256), R("BOb", 0, 256))
    act(L, R("BO4", 0, 256), R("BOb", 0, 256), 0.0, 4.0)
    act(L, R("ID2", 0, 256), R("IDf", 0, 256))
    fill(L, R("ID2", 0, 256, 16), 0.0)
    cp(L, R("IDa", 0, 256), R("ID2", 0, 256))
    tt(L, R("IDp", 0, 256), R("IDf", 0, 256), R("ID2", 0, 256), al.subtract)
    cp(L, R("IDh", 0, 256), R("IDf", 0, 256))
    cp(L, R("BOh", 0, 128), R("BOb", 0, 128))
    act(L, R("CKm", 0, 768), R("CK", 0, 768), 0.0, 32.0)
    act(L, R("CKa", 0, 768), R("CK", 0, 768), 0.0, 148.0)
    fill(L, R("SD", 0, 2048), 0.0)
    for x in range(16):
        cp(L, R("SD", 128 * x + x, 128 * x + 128, 16), R("BOb", 0, 128, 16))
    act(L, R("NEG", 0, 256), R("IDf", 0, 256), 0.0, -128.0)
    fill(L, R("HF", 0, 128), 0.5)
    fill(L, R("ZF", 0, 128), 0.0)
    op(L, "v", 0.12, [R("HF", 0, 128), R("ZF", 0, 128)], [R("PW", 0, 128)],
       lambda Q, A: [Q["v"].tensor_tensor_scan(out=A(R("PW", 0, 128)), data0=A(R("HF", 0, 128)), data1=A(R("ZF", 0, 128)),
                                               initial=float(2.0 ** 64), op0=al.mult, op1=al.add)])
    ts(L, R("b2", 256, 384), R("PW", 0, 128), 2.5, None, al.mult)
    mm(L, R("b7", 0, 2), [(R("PW", 0, 128, 1, 0, 1), R("OFm", 0, 2, 1, 0, 1))])
    cp(L, R("WC", 0, 2), R("b7", 0, 2))
    fill(L, R("Wq", 0, 1024), 0.0)
    for q in range(8):
        ts(L, R("Wq", 144 * q, 144 * q + 16), R("OB", 0, 16), R("WC", 0, 1), None, al.mult)
    mm(L, R("b7", 0, 384), [(R("I16", 0, 128), R("I16", 0, 384))])
    cp(L, R("ML", 0, 384), R("b7", 0, 384))
    for k in range(3):
        cp(L, R("CS", 8 * k, 8 * k + 8), R("BOf", 0, 128, 16))
    ts(L, R("XI", 0, 1), R("PX", 0, 1), 15, None, al.bitwise_and)
    cp(L, R("XF", 0, 1), R("XI", 0, 1))
    ts(L, R("IC", 0, 1), R("PX", 0, 1), 256.0, None, al.add)
    ts(L, R("IW", 0, 1), R("PX", 0, 1), 128.0, 2.0, al.add, al.mult)
    ts(L, R("DK", 0, 8), R("DLi", 0, 8), R("XF", 0, 1), None, al.add)
    ts(L, R("DK", 8, 16), R("DLi", 0, 8), R("XF", 0, 1), 128.0, al.add, al.add)
    fill(L, R("Z1", 0, 8), 0.0)
    cp(L, R("AD", 0, 8), R("Z1", 0, 8))
    ts(L, R("AD", 8, 16), R("Z1", 0, 8), 1.0, None, al.add)
    for k, b in ((0, 256.0), (1, 384.0), (2, 768.0)):
        ts(L, R("DL", 8 * k, 8 * k + 8), R("DLi", 0, 8), R("XF", 0, 1), b, al.add, al.add)
    asel(L, R("DT", 0, 128), R("OFm", 0, 128), [[-1, 128]], al.is_equal, 0.0, 1, 1)
    fill(L, R("DT", 0, 128, 16), 0.0)
    tt(L, R("HB", 0, 128), R("IDf", 0, 128), R("DT", 0, 128), al.subtract)
    act(L, R("MB", 0, 128), R("DT", 0, 128), 0.0, -8192.0)
    act(L, R("NI", 0, 128), R("IDf", 0, 128), 0.0, -1.0)
    fill(L, R("RY", 0, 128, 1, 0, 2), -1.0)
    fill(L, R("RY", 0, 128, 1, 0, 1), 2048.0)
    fill(L, R("RZ", 0, 128, 1, 0, 2), -1.0)
    fill(L, R("RZ", 0, 128, 1, 0, 1), 7936.0)
    ts(L, R("Z0", 0, 1), R("XF", 0, 1), 0.0, None, al.is_equal)
    ts(L, R("S1", 0, 1), R("Z0", 0, 1), -2.0, 1.0, al.mult, al.add)
    ts(L, R("S3", 0, 1), R("XF", 0, 1), -4.0, 68.0, al.mult, al.add)
    ts(L, R("Z1", 0, 1), R("Z0", 0, 1), -76.0, None, al.mult)
    tt(L, R("S2", 0, 1), R("S3", 0, 1), R("Z1", 0, 1), al.add)
    for k in range(4):
        fill(L, R("CR", 128 * k, 128 * k + 128), float(8 * k + 5))
        fill(L, R("CR", 512 + 128 * k, 640 + 128 * k), float(37 * k))
    for m in range(3):
        fill(L, R("CR", 1024 + 128 * m, 1152 + 128 * m), float(3 - m))
    fill(L, R("DS", 0, 128, 16), 0.0)
    fill(L, R("DS", 15, 128, 16), 0.0)
    tt(L, R("DM", 0, 128), R("IDf", 0, 128), R("DS", 0, 128), al.subtract)
    fill(L, R("RM", 0, 1024), 1.0)
    fill(L, R("RM", 0, 1024, 16), 0.0)


def offsets(L, k, src, mul, add):
    al = AluOpType
    a = lambda nm: R(nm, 128 * k, 128 * k + 128)
    tt(L, a("pi"), src, mul, al.mult)
    ts(L, a("pj"), a("pi"), 5, None, al.arith_shift_right)
    tt(L, a("pk"), a("pj"), add, al.add)
    ts(L, a("pl"), a("pk"), MASK, None, al.bitwise_and)
    ts(L, a("of"), a("pl"), 4096.0, None, al.min)


def look(L, k, win="tab"):
    al = AluOpType
    for h in range(2):
        a, b = 1024 * h, 1024 * h + 1024
        g, z = R("G", 2048 * k + a, 2048 * k + b), R("Z", 2048 * k + a, 2048 * k + b)
        gather(L, g, R(win, 0, 4112), R("of", 128 * k + 64 * h, 128 * k + 64 * h + 64), "vs")

        def emit(Q, A, g=g, z=z):
            return [Q["v"].tensor_tensor_scan(out=A(z), data0=A(R("RM", 0, 1024)), data1=A(g), initial=0.0, op0=al.mult, op1=al.max)]
        op(L, "v", 512 * CYC, [R("RM", 0, 1024), g], [z], emit)


def own_value(L, c, k, src, bank, out, win):
    offsets(L, k, src, R("MUS", 128 * c, 128 * c + 128), R("A3S", 128 * c, 128 * c + 128))
    look(L, k, win)
    mm(L, bank, [(R("BOb", 0, 128), R("Z", 2048 * k + 15, 2048 * k + 2048, 16))])
    act(L, out, bank)


def program(r, arrive):
    al = AluOpType
    L = []
    constants(L)
    gd = lambda q, out, in_, reads, writes, sem, ext, rel: op(
        L, q, 2.2, reads, writes, lambda Q, A: [Q[q].dma_start(out(A), in_(A))], sem=sem, ext=ext, rel=rel)
    gd("sy", lambda A: A(R("PI", 0, 128, 1, 0, 8)), lambda A: A("qr")[:, 16 * r:16 * r + 16, :], [], [R("PI", 0, 128, 1, 0, 8)], "d1",
       [("aq", arrive["aq"]), ("m10", 16)], 9.0)
    gd("ss", lambda A: A(R("tab", 0, 4096, 1, 16 * r, 16 * r + 16)), lambda A: A("sight")[16 * r:16 * r + 16, :], [],
       [R("tab", 0, 4096, 1, 16 * r, 16 * r + 16)], "d2", [], 2.0)
    for n, (s, cnt) in enumerate(arrive["x"]):
        gd("sy", lambda A, s=s: A(R("tab", 0, 4096, 1, 16 * s, 16 * s + 16)), lambda A, s=s: A("xr")[s], [],
           [R("tab", 0, 4096, 1, 16 * s, 16 * s + 16)], "d%d" % (3 + n), [("ax%d" % s, cnt)], 10.0 + n)
    op(L, "sy", 3.5, [], [R("BH", 0, 512)], lambda Q, A: [], sem="d21")
    op(L, "ss", 6.0, [], [R("tabH", 0, 4096)], lambda Q, A: [], sem="d22")
    ts(L, R("BU", 0, 512), R("BH", 0, 512), 1.0, None, al.add)
    gd("sy", lambda A: A("bs"), lambda A: A(R("BU", 0, 512)), [R("BU", 0, 512)], [R("bs", 0, 1)], "d0", [], 0.0)
    gd("sy", lambda A: A("br")[r], lambda A: A(R("BU", 0, 512, 1, 16 * r, 16 * r + 16)), [R("BU", 0, 512)], [R("br", 0, 1)], "d29", [], 0.0)
    L[op(L, "g", 1.5, [R("bs", 0, 1)], [R("bs", 1, 2)], lambda Q, A: Q["values"]("bs", "br", "ab"))]["boost"] = 1000
    gd("sy", lambda A: A(R("BI", 0, 512)), lambda A: A("br"), [R("br", 0, 1), R("bs", 1, 2)], [R("BI", 0, 512)], "m7", [("ab", arrive["ab"])], 2.5)
    ts(L, R("BB", 0, 512), R("BH", 0, 512), 0.0, 1.0 - OFF, al.is_lt, al.mult)
    tt(L, R("HC", 0, 512), R("BH", 0, 512), R("BB", 0, 512), al.add)
    for c in range(4):
        own_value(L, c, c, R("HC", c, 512, 4), R("b%d" % c, 0, 128), R("VH", 128 * c, 128 * c + 128), "tabH")
        if c in (0, 3):
            a, b = (0, 128) if c == 0 else (128, 512)
            x, y, z = ("vas", "var", "aa") if c == 0 else ("vhs", "vhr", "ah")
            k = 23 if c == 0 else 26
            gd("ss", lambda A, x=x, a=a, b=b: A(x), lambda A, x=x, a=a, b=b: A(R("VH", a, b))[0:128:16, :], [R("VH", a, b)], [R(x, 0, 1)],
               "d%d" % k, [], 0.0)
            gd("ss", lambda A, y=y: A(y)[r], lambda A, a=a, b=b: A(R("VH", a, b, 1, 16 * r, 16 * r + 1)), [R("VH", a, b)], [R(y, 0, 1)],
               "d%d" % (k + 1), [], 0.0)
            op(L, "g", 1.5, [R(x, 0, 1)], [R(x, 1, 2)], lambda Q, A, x=x, y=y, z=z: Q["values"](x, y, z))
            gd("sy", lambda A, a=a, b=b: A(R("V8", a, b, 1, 0, 8)), lambda A, y=y: A(y), [R(y, 0, 1), R(x, 1, 2)], [R("V8", a, b, 1, 0, 8)],
               "d%d" % (k + 2), [(z, N - 1)], 2.5)
    for c in range(4):
        mm(L, R("b%d" % (4 + c), 128, 256), [(R("S8", 0, 128, 1, 0, 8), R("V8", 128 * c, 128 * c + 128, 1, 0, 8))])
        act(L, R("F%d" % c, 128, 256), R("b%d" % (4 + c), 128, 256))
    cp(L, R("BF", 0, 512), R("BI", 0, 512))
    ts(L, R("BA", 0, 512), R("BF", 0, 512), 0.0, 1.0 - OFF, al.is_equal, al.mult)
    tt(L, R("BT", 0, 512), R("BF", 0, 512), R("BA", 0, 512), al.add)
    for c in range(4):
        mm(L, R("b%d" % (4 + c), 0, 128), [(R("REV", 0, 128), R("BT", c, 512, 4))])
        act(L, R("F%d" % c, 0, 128), R("b%d" % (4 + c), 0, 128), -1.0)
    p8 = lambda nm: R(nm, 0, 128, 1, 0, 8)
    ts(L, p8("PB"), p8("PI"), 0.0, 1.0 - OFF, al.is_lt, al.mult)
    tt(L, p8("PC"), p8("PI"), p8("PB"), al.add)
    mm(L, R("b3", 0, 128), [(p8("S8"), p8("PC"))])
    ts(L, R("P0", 0, 128), R("b3", 0, 128), -SH, None, al.add)
    marks = []
    tile = ["F%d" % c for c in range(4)]
    for t in range(4):
        marks.append(len(L))
        F = tile[t]
        FB, FV = R(F, 0, 128), R(F, 128, 256)
        cl = [(t + 1 + m) % 4 for m in range(3)]
        dl = [0, 1 + t, 2 + t]
        fwd = lambda nm, m: R(nm, 128 - 16 * dl[m], 256 - 16 * dl[m])
        bwd = lambda nm, m: R(nm, 16 * dl[m], 16 * dl[m] + 128)
        ckf = lambda nm, w, m: R(nm, 256 * w + 128 - 16 * dl[m], 256 * w + 256 - 16 * dl[m])
        bk = lambda b, m: R("b%d" % b, 128 * m, 128 * m + 128)
        at = lambda nm, m, w=128: R(nm, w * m, w * m + w)
        P = R("P%d" % t, 0, 128)
        tt(L, R("kS", 0, 128), FB, FV, al.add)
        if t:
            ts(L, R("kT", 0, 128), R("kS", 0, 128), float(13 * t), None, al.add)
        ts(L, R("kU", 0, 128), R("kT" if t else "kS", 0, 128), 127, None, al.bitwise_and)
        cp(L, R("kL", 0, 128), R("kU", 0, 128))
        kL = R("kL", 0, 128)
        row = lambda a: R("CR", a, a + 128, 1, 0, 1)
        one = R("OB", 0, 128, 1, 0, 1)
        Fh = R("Fh", 0, 128)
        ts(L, Fh, FB, -SH, None, al.add)
        for m in range(3):
            mm(L, bk(4 + m, 2), [(fwd("IDp", m), P), (fwd("IDa", m), Fh)])
            sx = at("SX", m)
            act(L, sx, bk(4 + m, 2), SH)
            mm(L, bk(1 + m, 0), [(one, row(128 * cl[m])), (ckf("CKm", m, m), kL)])
            mm(L, bk(1 + m, 1), [(one, row(512 + 128 * cl[m])), (ckf("CKa", m, m), kL)])
            offsets(L, m, sx, bk(1 + m, 0), bk(1 + m, 1))
            look(L, m)
        mm(L, bk(2, 3), [(R("DM", 0, 128), Fh)])
        for m in range(3):
            mm(L, bk(0, m), [(R("RI", 0, 128, 1, 0, 2), R("OB", 0, 128, 1, 0, 2)), (kL, ckf("CK", m, m))])
        op(L, "s", 0.12, [R("b0", 0, 384, 16), R("IC", 0, 1)], [R("KTs", 0, 24)], lambda Q, A: [Q["s"].activation(
            out=A(R("KTs", 0, 24)), in_=A(R("b0", 0, 384, 16)), func=ActivationFunctionType.Identity, bias=A(R("IC", 0, 1)), scale=1.0)])
        for m in range(3):
            tt(L, at("KM", m), bk(0, m), at("ML", m), al.mult)
            mm(L, R("b0", 384 + 24 * m, 408 + 24 * m), [(at("KM", m), R("CS", 0, 24)), (R("IDh", 0, 128), R("DL", 0, 24))])
        cp(L, R("LK", 0, 72), R("b0", 384, 456))
        for m in range(3):
            for h in range(2):
                def emit(Q, A, m=m, h=h):
                    return [Q["v"].tensor_scalar(out=A(R("EH", 1024 * m + 128 * q, 1024 * m + 128 * q + 128)), in0=A(R("IOK", 0, 128)),
                                                 scalar1=A(R("KTs", 8 * m + q, 8 * m + q + 1)), scalar2=None, op0=al.is_equal)
                            for q in range(4 * h, 4 * h + 4)]
                op(L, "v", 4 * 64 * CYC, [R("IOK", 0, 128), R("KTs", 8 * m + 4 * h, 8 * m + 4 * h + 4)],
                   [R("EH", 1024 * m + 512 * h, 1024 * m + 512 * h + 512)], emit, n=4)
            mm(L, R("b%d" % (4 + m), 384, 512),
               [(R("Wq", 128 * q, 128 * q + 128), R("EH", 1024 * m + 128 * q, 1024 * m + 128 * q + 128)) for q in range(8)])
            Fc = tile[cl[m]]
            act(L, R(Fc, 512, 640), R("b%d" % (4 + m), 384, 512))
            gather(L, at("R", m, 384), R(Fc, 0, 640), R("LK", 24 * m, 24 * m + 24), "s")
            tt(L, at("NF", m), R("R", 384 * m + 256, 384 * m + 384), R("b2", 256, 384), al.is_ge)
        for m in range(3):
            sv, mk, nv, hot = [R("b%d" % (4 + m), 128 * k, 128 * k + 128) for k in range(4)]
            for h in (0, 64):
                mm(L, sub(sv, h, h - 64), [(R("SD", 128 * x, 128 * x + 128), R("Z", 2048 * m + 16 * h + x, 2048 * m + 16 * h + 1024, 16))
                                           for x in range(16)])
            tt(L, at("IN", m), sv, R("R", 384 * m + 128, 384 * m + 256), al.is_gt)
            mm(L, bk(7, m), [(one, row(1024 + 128 * m)), (bwd("BO4", m), at("IN", m)), (bwd("NEG", m), at("NF", m))])
            act(L, at("SVs", m), sv, -2040.0)
            mm(L, mk, [(R("RZ", 0, 128, 1, 0, 2), R("OB", 0, 128, 1, 0, 2)), (R("MB", 0, 128), at("IN", m))])
            mm(L, hot, [(R("HB", 0, 128), at("IN", m))])
            tt(L, R(tile[cl[m]], 256, 512, 2), mk, at("SX", m), al.min)
            tt(L, at("HS", m), hot, at("SVs", m), al.mult)
            mm(L, nv, [(R("BOh", 0, 128), at("HS", m))])
            act(L, R(tile[cl[m]], 257, 512, 2), nv, 2040.0)
        ts(L, at("KB", 0), bk(7, 0), 3.25, None, al.max)
        tt(L, at("KB", 1), at("KB", 0), bk(7, 1), al.max)
        tt(L, at("KB", 2), at("KB", 1), bk(7, 2), al.max)
        kb = at("KB", 2)
        for m in range(3):
            tt(L, at("WB", m), kb, bk(7, m), al.is_equal)
            mm(L, bk(1 + m, 0), [(at("WB", m), ckf("CK", 0, m))])
            ts(L, at("WK", m), bk(1 + m, 0), R("IW", 0, 1), None, al.mult)
            mms(L, bk(1 + m, 1), [(R("EH", 1024 * m + 128 * q, 1024 * m + 128 * q + 128), R("WK", 128 * m + 16 * q, 128 * m + 16 * q + 16)) for q in range(8)])
            tt(L, at("MJ", m), bk(1 + m, 1), at("ML", m), al.mult)
            b16 = R("b0", 384 + 16 * m, 400 + 16 * m)
            mm(L, b16, [(at("MJ", m), R("CS", 0, 16)), (R("IDh", 0, 128), R("AD", 0, 16))])
            tt(L, at("LX", m, 16), b16, R("DK", 0, 16), al.max)
            cp(L, at("LW", m, 16), at("LX", m, 16))
            new = tile[cl[m]].replace("F", "e").replace("E", "F").replace("e", "E")
            gather(L, R(new, 0, 256), R(tile[cl[m]], 0, 512), at("LW", m, 16), "s")
            tile[cl[m]] = new
        ts(L, R("H1", 0, 128), kb, R("S1", 0, 1), R("S2", 0, 1), al.mult, al.is_gt)
        tt(L, R("HD", 0, 128), R("H1", 0, 128), bk(2, 3), al.mult)
        mm(L, bk(7, 0), [(R("BOf", 112, 240), R("HD", 0, 128))])
        cp(L, R("P%d" % (t + 1), 0, 128), bk(7, 0))
        for m in range(4):
            act(L, at("RH", m), at("R", m, 384)[:2] + (384 * m + 128, 1, 0, 128) if m < 3 else at("SX", 0), -SH)
        mm(L, bk(5, 1), [(one, R("OB", 0, 128, 1, 0, 1))] + [(R("NI", 0, 128), at("WB", m)) for m in range(3)])
        tt(L, at("TH", 3), bk(5, 1), at("RH", 3), al.mult)
        for m in range(3):
            mm(L, bk(4 + m, 0), [(fwd("IDb", m), at("WB", m))])
            tt(L, at("TH", m), bk(4 + m, 0), at("RH", m), al.mult)
        mm(L, bk(3, 2), [(R("RY", 0, 128, 1, 0, 2), R("OB", 0, 128, 1, 0, 2)), (R("IDh", 0, 128), at("TH", 3))]
           + [(bwd("IDh", m), at("TH", m)) for m in range(3)])
        act(L, FB, bk(3, 2))
        own_value(L, t, 3, bk(3, 2), bk(7, 3), FV, "tab")
    marks.append(len(L))
    for c in range(4):
        mm(L, R("b%d" % (4 + c), 0, 128), [(R("REV", 0, 128), R(tile[c], 0, 128))])
        ts(L, R("Y", c, 512, 4), R("b%d" % (4 + c), 0, 128), -1.0, None, al.max)
        act(L, R("VY", c, 512, 4), R(tile[c], 128, 256))
    ts(L, R("PO", 0, 128), R("P4", 0, 128), SH, -1.0, al.add, al.max)
    e = {}
    e["y"] = gd("sy", lambda A: A("ys"), lambda A: A(R("Y", 0, 512)), [R("Y", 0, 512)], [], "d12", [], 0.0)
    e["w"] = gd("sy", lambda A: A("ws"), lambda A: A(R("PO", 0, 128, 1, 0, 128))[0:128:16, :], [R("PO", 0, 128)], [], "d13", [], 0.0)
    gd("sy", lambda A: A("yr")[r], lambda A: A(R("Y", 0, 512, 1, 16 * r, 16 * r + 16)), [R("Y", 0, 512)], [], "d14", [], 0.0)
    gd("sy", lambda A: A("wr")[r], lambda A: A(R("PO", 0, 128, 1, 16 * r, 16 * r + 1)), [R("PO", 0, 128)], [], "d15", [], 0.0)
    e["v"] = gd("sy", lambda A: A("vs"), lambda A: A(R("VY", 0, 512))[0:128:16, :], [R("VY", 0, 512)], [], "d16", [], 0.0)
    gd("sy", lambda A: A("vr")[r], lambda A: A(R("VY", 0, 512, 1, 16 * r, 16 * r + 1)), [R("VY", 0, 512)], [], "d17", [], 0.0)
    return L, marks


def plan(T, topo):
    cores = [int(c) for c in T.cores]
    out = {}
    for r, c in enumerate(cores):
        mate = [s for s in range(N) if s != r and topo.chip(cores[s]) == topo.chip(c)]
        away = [s for s in range(N) if topo.chip(cores[s]) != topo.chip(c)]
        here = [s for s in range(N) if topo.chip(cores[s]) == topo.chip(c)]
        cand = [h for h in topo.cores_of(c) if topo.die(h) != topo.die(c) and h not in cores and all(topo.may_write(h, cores[s]) for s in away)]
        k = here.index(r)
        chips = sorted(set(topo.chip(cores[s]) for s in away))
        direct, helped = [], []
        for ch in chips:
            two_ = [s for s in away if topo.chip(cores[s]) == ch]
            direct.append(two_[k % 2])
            helped.append(two_[(k + 1) % 2])
        out[r] = {"mate": mate[0], "away": away, "direct": direct, "helped": helped, "helper": cand[k]}
    return cores, out


def bits(es):
    return sum(1 << int(x) for x in es)


def groups(p, r, cores, topo):
    me = cores[r]
    off = topo.engines(me, cores[p["away"][0]])
    on = [x for x in topo.engines(me, cores[p["mate"]]) if x not in off]
    a = [(s, off[2 * k:2 * k + 2]) for k, s in enumerate(p["away"][:4])] + [(p["mate"], on)]
    b = [(s, off[4 * k:4 * k + 4]) for k, s in enumerate(p["away"][4:6])]
    return [a, b], [[(s, off[k:k + 1]) for k, s in enumerate(p["away"])] + [(p["mate"], on[:1])]]


def rank_program(g, core, T, topo):
    cores, pl = plan(T, topo)
    rank = T.rank_of(core)
    addr = lambda c: topo.addr(c)[:2]

    def write(dst, o, i, rs, es):
        rid, pid = addr(dst)
        g.remote_dma(out_ap=o, in_ap=i, remote_sem=T.sem[rs], local_sem=T.sem["ls"], pid=pid, routing_id=rid, dma_engine_mask=bits(es))
        return len(es)

    if rank is None:
        for r in range(N):
            p = pl[r]
            if p["helper"] != core:
                continue
            n = 0
            for k, s in enumerate(p["helped"]):
                es = topo.engines(core, cores[s])
                on = [x for x in topo.engines(cores[r], core) if x not in topo.engines(cores[r], cores[s])]
                g.wait_ge(T.sem["hx%d" % k], len(on))
                n += write(cores[s], T["xr"][r], T["xr"][k], "ax%d" % r, es)
            g.wait_ge(T.sem["ls"], n)
        return

    r, p = rank, pl[rank]
    off = topo.engines(core, cores[p["away"][0]])
    on = [x for x in topo.engines(core, cores[p["mate"]]) if x not in off]
    many, single = groups(p, r, cores, topo)

    def cnt(s, d, which):
        for call in groups(pl[s], s, cores, topo)[which]:
            for dd, es in call:
                if dd == d:
                    return len(es)

    others = [s for s in range(N) if s != r]
    arrive = {"ab": len(others), "aq": len(others)}
    first = [s for s in others if s == p["mate"] or r in pl[s]["direct"]]
    late = len(topo.engines(p["helper"], cores[p["away"][0]]))
    arrive["x"] = [(s, len(on) if s == p["mate"] else late) for s in first + [s for s in others if s not in first]]

    seq = []
    for k in range(3):
        seq += [("h", p["helped"][k], k), ("d", p["direct"][k], k)]
    seq.append(("m", p["mate"], 3))
    for n, (kind, s, k) in enumerate(seq):
        q = (g.sync, g.scalar)[n % 2]
        q.dma_start(T["xs"][s], T["sight"][16 * s:16 * s + 16, :]).then_inc(T.sem["m%d" % n], 16)
        if n == 0:
            g.sync.dma_start(T["BH"][:], T["bun"][:]).then_inc(T.sem["d21"], 16)
        if n == 1:
            g.scalar.dma_start(T["tabH"][:, 0:4096], T["sight"][:]).then_inc(T.sem["d22"], 16)
        if n == 6:
            g.scalar.dma_start(T["qs"][:], T["pots"][:]).then_inc(T.sem["m8"], 16)
            g.scalar.dma_start(T["qr"][r], T["pots"][:]).then_inc(T.sem["m10"], 16)
    tot = {}
    loc = [0]

    def fused(calls, src, dst, sem):
        for call in calls:
            tr = []
            for s, es in call:
                rid, pid = addr(cores[s])
                tr.append(RemoteDMATransfer(dst_ids=[DstId(rid=rid, pnc=pid)], dma_engine_mask=bits(es), remote_sem=T.sem[sem],
                                            src=T[src][s], dst=T[dst][r]))
                loc[0] += len(es)
            g.remote_dma_fused(tr, local_sem=T.sem["ls"])

    def exchange():
        for part in range(4):
            tr = []
            for n, (kind, s, k) in enumerate(seq):
                if k == part:
                    g.wait_ge(T.sem["m%d" % n], 16)
                    c, slot, sem = (p["helper"], k, "hx%d" % k) if kind == "h" else (cores[s], r, "ax%d" % r)
                    es = off if kind == "d" else on
                    rid, pid = addr(c)
                    tr.append(RemoteDMATransfer(dst_ids=[DstId(rid=rid, pnc=pid)], dma_engine_mask=bits(es), remote_sem=T.sem[sem],
                                                src=T["xs"][s], dst=T["xr"][slot]))
                    loc[0] += len(es)
            g.remote_dma_fused(tr, local_sem=T.sem["ls"])
        g.wait_ge(T.sem["m8"], 16)
        ids, ds = [], []
        for d in others:
            rid, pid = addr(cores[d])
            ids.append(DstId(rid=rid, pnc=pid))
            ds.append(T["qr"][r])
        g.remote_dma_fused([RemoteDMATransfer(dst_ids=ids, dma_engine_mask=bits(off[:1]), remote_sem=T.sem["aq"], srcs=[T["qs"][:]], dsts=ds)],
                           local_sem=T.sem["ls"])
        loc[0] += 1
        return []

    L, marks = program(r, arrive)
    depend(L)
    order, busy = schedule(L, marks)
    def values(a, b, s):
        fused(single, a, b, s)
        return []

    Q = {"exchange": exchange, "values": values, "v": g.vector, "s": g.scalar, "pe": g.tensor, "g": g, "sy": g.sync, "ss": g.scalar, "who": [None]}

    def A(x):
        if isinstance(x, str):
            return T[x][:]
        nm, c0, c1, st, p0, p1 = x
        return T[nm][p0:p1, c0:c1] if st == 1 else T[nm][p0:p1, c0:c1:st]
    emit_all(L, order, Q, A, T, tot)

    g.wait_ge(T.sem["d13"], 16)
    fused(single, "ws", "wr", "aw")
    g.wait_ge(T.sem["d12"], 16)
    fused(many, "ys", "yr", "ay")
    g.wait_ge(T.sem["d16"], 16)
    fused(single, "vs", "vr", "av")
    g.sync.wait_ge(T.sem["d14"], 16)
    g.sync.wait_ge(T.sem["ay"], sum(cnt(s, r, 0) for s in others))
    g.sync.dma_start(T["yb"][:], T["yr"][:]).then_inc(T.sem["d18"], 16)
    g.sync.wait_ge(T.sem["d15"], 16)
    g.sync.wait_ge(T.sem["aw"], len(others))
    g.sync.dma_start(T["yp"][:], T["wr"][:]).then_inc(T.sem["d19"], 16)
    g.sync.wait_ge(T.sem["d17"], 16)
    g.sync.wait_ge(T.sem["av"], len(others))
    g.sync.dma_start(T["yv"][:], T["vr"][:]).then_inc(T.sem["d20"], 16)
    for s in sorted(tot):
        g.wait_ge(T.sem[s], tot[s])
    g.wait_ge(T.sem["ls"], loc[0])
    for s in ("d18", "d19", "d20"):
        g.wait_ge(T.sem[s], 16)
